import numpy as np
import ml_dtypes


def mxq(x, axis, fmt="e4m3"):
    dtype, down = {"e4m3": (ml_dtypes.float8_e4m3fn, 7), "e5m2": (ml_dtypes.float8_e5m2, 14)}[fmt]
    v = np.moveaxis(np.asarray(x, np.float32).astype(ml_dtypes.bfloat16).astype(np.float64), axis, -1)
    blocks = v.reshape(v.shape[:-1] + (-1, 32))
    amax = np.abs(blocks).max(-1, keepdims=True)
    byte = np.maximum(np.where(amax > 0, np.frexp(amax)[1] - 1 + 127, 0) - down, 1)
    scale = np.exp2(byte - 127.0)
    codes = (blocks / scale).astype(np.float32).astype(dtype).astype(np.float64)
    return np.moveaxis((codes * scale).reshape(v.shape), -1, axis)


WIDE = False


def mx_kscale(k):
    if not WIDE:
        return np.ones(k)
    levels = np.array([10, -10, 5, -5, 0])
    if k % 512:
        return np.exp2(np.random.permutation(np.resize(levels, k // 32))).repeat(32)
    a = np.empty((k // 512, 16))
    for p in range(k // 512):
        a[p, :8] = np.random.permutation(np.resize(levels, 8))
        for g in range(8):
            far = levels[np.abs(levels - a[p, g]) >= 10]
            a[p, g + 8] = far[np.random.randint(len(far))]
    return np.exp2(a.ravel()).repeat(32)


def f64(x):
    return np.asarray(x).astype(np.float64)


def striped(idx):
    return np.tile(idx.reshape(-1, 16).T, (8, 1)).astype(np.uint16)


def unstriped(offs):
    return offs[:16].T.reshape(-1).astype(np.int64)


def pack_weight(w):
    k, n = w.shape
    w = f64(np.asarray(w, np.float32).astype(ml_dtypes.bfloat16)).reshape(k // 32, 32, n)
    amax = np.abs(w).max(1)
    byte = np.clip(np.where(amax > 0, np.frexp(amax)[1] - 1 + 127 - 7, 1), 1, 254)
    scaled = (w * np.exp2(127.0 - byte)[:, None, :]).reshape(k, n).astype(np.float32)
    words = np.ascontiguousarray(scaled.reshape(k // 512, 128, 4, n).transpose(0, 1, 3, 2)).astype(ml_dtypes.float8_e4m3fn).view(np.uint8)
    return words, np.ascontiguousarray(byte.astype(np.uint8).reshape(k // 512, 16, n))


def unpack_weight(words, scales):
    g, p, n, _ = words.shape
    vals = np.ascontiguousarray(words).view(ml_dtypes.float8_e4m3fn).astype(np.float64) * np.repeat(np.exp2(scales.astype(np.float64) - 127.0), 8, axis=1)[..., None]
    return vals.transpose(0, 1, 3, 2).reshape(g * 512, n)


def silu(v):
    return v / (1.0 + np.exp(-np.maximum(v, -700.0)))


K, T, D, S, V, N = 512, 1024, 2, 1024, 512, 128


def setup_inputs():
    n = np.random.standard_normal
    s = mx_kscale(K)[:, None]
    words, scales = pack_weight(n((K, N)) / np.sqrt(K) / s)
    return {
        "xT": (n((K, T)) * s / np.sqrt(D)).astype(ml_dtypes.bfloat16).astype(np.float32),
        "w_words": words,
        "w_scales": scales,
        "b": (0.3 * n((N, 1))).astype(np.float32),
        "offs": striped(np.concatenate([np.random.permutation(T)[:V] for _ in range(D)])),
    }


def reference(xT, w_words, w_scales, b, offs):
    w = unpack_weight(w_words, w_scales)
    idx = unstriped(offs)
    x = sum(f64(xT)[:, idx[d * V:(d + 1) * V]] for d in range(D))
    return silu((w.T @ mxq(x, 0, "e4m3")) + f64(b))

@@ -1,0 +1,128 @@
+from contextlib import ExitStack
+
+import concourse.mybir as mybir
+
+K, T, D, V, N = 512, 1024, 2, 512, 128
+FLOPS = 2 * K * V * N
+
+F32 = mybir.dt.float32
+BF16 = mybir.dt.bfloat16
+I32 = mybir.dt.int32
+U32 = mybir.dt.uint32
+U16 = mybir.dt.uint16
+U8 = mybir.dt.uint8
+FP8X4 = mybir.dt.float8_e4m3fn_x4
+ACT = mybir.ActivationFunctionType
+ADD = mybir.AluOpType.add
+
+P = 128
+FIRST_CUTS = [768,256]
+PAIR_CUTS = [512,256,256]
+LAST_CUTS = [512,512]
+ID_CUTS = [256,128,128]
+
+
+def spans(widths):
+    starts = [sum(widths[:i]) for i in range(len(widths))]
+    return [(s, s + w) for s, w in zip(starts, widths)]
+
+
+def tile_picked_hash_lin_silu_sub_l_kernel(tc, xT, w_words, w_scales, b, offs, out):
+    nc = tc.nc
+    with ExitStack() as ctx:
+        pool = ctx.enter_context(tc.tile_pool(name="held", bufs=1))
+        psum = ctx.enter_context(tc.psum_pool(name="psum", bufs=1))
+
+        planes = xT.rearrange("(p t) c -> p t c", t=4)
+        offsets = pool.tile([P, D * V // 16], U16, name="offsets")
+
+        warm_in = pool.tile([P, 1], F32, name="warm_in")
+        warm_out = pool.tile([P, 1], F32, name="warm_out")
+        w_scale = pool.tile([P, N], U8, name="w_scale", align_bytes=64)
+        nc.vector.memset(warm_in[:], 0.0)
+        nc.vector.memset(w_scale[:].bitcast(I32), 0)
+        nc.scalar.activation(warm_out[:], warm_in[:], ACT.Silu)
+
+        def load(name, src, shape):
+            raw = pool.tile(shape, F32, name=name)
+            nc.sync.dma_start(raw[:], src)
+            return raw
+
+        raw0 = [load("raw0_%d" % a, planes[:, 0, a:z], [P, z - a]) for a, z in spans(FIRST_CUTS)]
+        nc.sync.dma_start(offsets[:], offs)
+        raw23 = [load("raw23_%d" % a, planes[:, 2:4, a:z], [P, 2, z - a]) for a, z in spans(PAIR_CUTS)]
+        picked = pool.tile([P, 2, D, V], U32, name="picked")
+        own = pool.tile([P, LAST_CUTS[0]], F32, name="raw1_own")
+        zone = picked[:, 1].rearrange("p d v -> p (d v)").bitcast(F32)
+        raw1 = [own[:], zone[:, 384:896]]
+        for raw, (a, z) in zip(raw1, spans(LAST_CUTS)):
+            nc.sync.dma_start(raw, planes[:, 1, a:z])
+
+        w_codes = pool.tile([P, N], U32, name="w_codes", align_bytes=64)
+        nc.sync.dma_start(w_codes[:].bitcast(I32), w_words[0].rearrange("p n r -> p (n r)").bitcast(I32))
+        for q in range(4):
+            nc.sync.dma_start(w_scale[32 * q : 32 * q + 4, :].bitcast(I32), w_scales[0, 4 * q : 4 * q + 4, :].bitcast(I32))
+        bias = pool.tile([P, 1], F32, name="bias")
+        nc.sync.dma_start(bias[:], b)
+
+        win0 = pool.tile([P, T], BF16, name="win0")
+        win1 = pool.tile([P, T], BF16, name="win1")
+        win23 = pool.tile([P, T], U32, name="win23")
+
+        def list_slice(d, a, z):
+            return offsets[:, (d * V + a) // 16 : (d * V + z) // 16]
+
+        def gather_half(window, e, a, z):
+            for d in range(D):
+                dst = picked[:, 0, d, a:z].bitcast(BF16).rearrange("p (v e) -> p v e", e=2)[:, :, e]
+                nc.scalar.activation(dst, window[:].indirect(list_slice(d, a, z)), ACT.Copy)
+
+        for raw, (a, z) in zip(raw0, spans(FIRST_CUTS)):
+            nc.vector.tensor_copy(win0[:, a:z], raw[:])
+        for raw, (a, z) in zip(raw23, spans(PAIR_CUTS)):
+            dst = win23[:, a:z].bitcast(BF16).rearrange("p (c e) -> p c e", e=2)
+            nc.vector.tensor_copy(dst, raw[:].rearrange("p e c -> p c e"))
+        gather_half(win0, 0, 0, V)
+
+        def gather_words(d, a, z):
+            nc.vector.tensor_copy(picked[:, 1, d, a:z], win23[:].indirect(list_slice(d, a, z)))
+
+        def cast_last(i, copy):
+            a, z = spans(LAST_CUTS)[i]
+            copy(win1[:, a:z], raw1[i])
+
+        cast_last(0, nc.scalar.copy)
+        gather_words(0, 0, 256)
+        cast_last(1, nc.vector.tensor_copy)
+        gather_words(1, 0, 256)
+        gather_words(0, 256, 512)
+        gather_words(1, 256, 512)
+        for a, z in spans(ID_CUTS):
+            gather_half(win1, 1, a, z)
+
+        sums = [pool.tile([P, 4 * w], BF16, name="sum_%d" % c, align_bytes=64) for c, w in enumerate(ID_CUTS)]
+
+        def add(c):
+            a, z = spans(ID_CUTS)[c]
+            rows = [picked[:, :, d, a:z].bitcast(BF16).rearrange("p u (v e) -> p v u e", e=2) for d in range(D)]
+            nc.vector.tensor_tensor(sums[c][:].rearrange("p (v u e) -> p v u e", u=2, e=2), rows[0], rows[1], ADD)
+
+        def finish(c):
+            a, z = spans(ID_CUTS)[c]
+            codes = pool.tile([P, z - a], U32, name="codes_%d" % c, align_bytes=64)
+            scale = pool.tile([P, z - a], U8, name="scale_%d" % c, align_bytes=64)
+            nc.vector.quantize_mx(out=codes[:].bitcast(FP8X4), scales=scale[:], in_=sums[c][:])
+            acc = psum.tile([P, z - a], F32, name="acc_%d" % c)
+            nc.tensor.matmul_mx(
+                out=acc[:], lhsT=w_codes[:].bitcast(FP8X4), lhsT_scale=w_scale[:],
+                rhs=codes[:].bitcast(FP8X4), rhs_scale=scale[:], start=True, stop=True,
+            )
+            result = pool.tile([P, z - a], F32, name="result_%d" % c)
+            nc.scalar.activation(result[:], acc[:], ACT.Silu, bias=bias[:])
+            nc.sync.dma_start(out[:, a:z], result[:])
+
+        add(0)
+        for c in range(1, len(ID_CUTS)):
+            add(c)
+            finish(c - 1)
+        finish(len(ID_CUTS) - 1)

@@ -16,9 +16,10 @@ ACT = mybir.ActivationFunctionType
 ADD = mybir.AluOpType.add
 
 P = 128
-FIRST_CUTS = [768,256]
+FIRST_CUTS = [1024]
 PAIR_CUTS = [512,256,256]
-LAST_CUTS = [512,512]
+LAST_CUTS = [256,256,256,256]
+SPLIT = 256
 ID_CUTS = [256,128,128]
 
 
@@ -48,15 +49,13 @@ def tile_picked_hash_lin_silu_sub_l_kernel(tc, xT, w_words, w_scales, b, offs, o
             nc.sync.dma_start(raw[:], src)
             return raw
 
-        raw0 = [load("raw0_%d" % a, planes[:, 0, a:z], [P, z - a]) for a, z in spans(FIRST_CUTS)]
+        raw0 = load("raw0", planes[:, 0, :], [P, T])
         nc.sync.dma_start(offsets[:], offs)
-        raw23 = [load("raw23_%d" % a, planes[:, 2:4, a:z], [P, 2, z - a]) for a, z in spans(PAIR_CUTS)]
-        picked = pool.tile([P, 2, D, V], U32, name="picked")
-        own = pool.tile([P, LAST_CUTS[0]], F32, name="raw1_own")
-        zone = picked[:, 1].rearrange("p d v -> p (d v)").bitcast(F32)
-        raw1 = [own[:], zone[:, 384:896]]
-        for raw, (a, z) in zip(raw1, spans(LAST_CUTS)):
-            nc.sync.dma_start(raw, planes[:, 1, a:z])
+        raw23 = pool.tile([P, 2, T], F32, name="raw23")
+        nc.sync.dma_start(raw23[:, 0, :], planes[:, 2, :])
+        for a, z in spans(PAIR_CUTS):
+            nc.sync.dma_start(raw23[:, 1, a:z], planes[:, 3, a:z])
+        raw1 = [load("raw1_%d" % a, planes[:, 1, a:z], [P, z - a]) for a, z in spans(LAST_CUTS)]
 
         w_codes = pool.tile([P, N], U32, name="w_codes", align_bytes=64)
         nc.sync.dma_start(w_codes[:].bitcast(I32), w_words[0].rearrange("p n r -> p (n r)").bitcast(I32))
@@ -66,45 +65,48 @@ def tile_picked_hash_lin_silu_sub_l_kernel(tc, xT, w_words, w_scales, b, offs, o
         nc.sync.dma_start(bias[:], b)
 
         win0 = pool.tile([P, T], BF16, name="win0")
-        win1 = pool.tile([P, T], BF16, name="win1")
+        win1 = raw0[:, 0 : T // 2].bitcast(BF16)
         win23 = pool.tile([P, T], U32, name="win23")
+        picked = pool.tile([P, D, 2, V], U32, name="picked")
 
         def list_slice(d, a, z):
             return offsets[:, (d * V + a) // 16 : (d * V + z) // 16]
 
-        def gather_half(window, e, a, z):
-            for d in range(D):
-                dst = picked[:, 0, d, a:z].bitcast(BF16).rearrange("p (v e) -> p v e", e=2)[:, :, e]
-                nc.scalar.activation(dst, window[:].indirect(list_slice(d, a, z)), ACT.Copy)
+        def half_words(e, d, a, z):
+            return picked[:, d, 0, a:z].bitcast(BF16).rearrange("p (v e) -> p v e", e=2)[:, :, e]
 
-        for raw, (a, z) in zip(raw0, spans(FIRST_CUTS)):
-            nc.vector.tensor_copy(win0[:, a:z], raw[:])
-        for raw, (a, z) in zip(raw23, spans(PAIR_CUTS)):
+        def gather_half(window, e, d, a, z):
+            nc.scalar.activation(half_words(e, d, a, z), window.indirect(list_slice(d, a, z)), ACT.Copy)
+
+        for copy, (a, z) in zip((nc.vector.tensor_copy, nc.scalar.copy), spans(FIRST_CUTS)):
+            copy(win0[:, a:z], raw0[:, a:z])
+        nc.vector.tensor_copy(half_words(0, 1, SPLIT, V), raw0[:].indirect(list_slice(1, SPLIT, V)))
+        for a, z in spans(PAIR_CUTS):
             dst = win23[:, a:z].bitcast(BF16).rearrange("p (c e) -> p c e", e=2)
-            nc.vector.tensor_copy(dst, raw[:].rearrange("p e c -> p c e"))
-        gather_half(win0, 0, 0, V)
+            nc.vector.tensor_copy(dst, raw23[:, :, a:z].rearrange("p e c -> p c e"))
+        gather_half(win0[:], 0, 0, 0, V)
+        gather_half(win0[:], 0, 1, 0, SPLIT)
 
         def gather_words(d, a, z):
-            nc.vector.tensor_copy(picked[:, 1, d, a:z], win23[:].indirect(list_slice(d, a, z)))
+            nc.vector.tensor_copy(picked[:, d, 1, a:z], win23[:].indirect(list_slice(d, a, z)))
 
         def cast_last(i, copy):
             a, z = spans(LAST_CUTS)[i]
-            copy(win1[:, a:z], raw1[i])
+            copy(win1[:, a:z], raw1[i][:])
 
-        cast_last(0, nc.scalar.copy)
-        gather_words(0, 0, 256)
-        cast_last(1, nc.vector.tensor_copy)
-        gather_words(1, 0, 256)
-        gather_words(0, 256, 512)
-        gather_words(1, 256, 512)
+        for i in range(len(LAST_CUTS)):
+            cast_last(i, nc.scalar.copy)
+        for d in range(D):
+            gather_words(d, 0, V)
         for a, z in spans(ID_CUTS):
-            gather_half(win1, 1, a, z)
+            for d in range(D):
+                gather_half(win1, 1, d, a, z)
 
         sums = [pool.tile([P, 4 * w], BF16, name="sum_%d" % c, align_bytes=64) for c, w in enumerate(ID_CUTS)]
 
         def add(c):
             a, z = spans(ID_CUTS)[c]
-            rows = [picked[:, :, d, a:z].bitcast(BF16).rearrange("p u (v e) -> p v u e", e=2) for d in range(D)]
+            rows = [picked[:, d, :, a:z].bitcast(BF16).rearrange("p u (v e) -> p v u e", e=2) for d in range(D)]
             nc.vector.tensor_tensor(sums[c][:].rearrange("p (v u e) -> p v u e", u=2, e=2), rows[0], rows[1], ADD)
 
         def finish(c):

@@ -16,10 +16,10 @@ ACT = mybir.ActivationFunctionType
 ADD = mybir.AluOpType.add
 
 P = 128
-FIRST_CUTS = [1024]
+FIRST_CUTS = [640,384]
 PAIR_CUTS = [512,256,256]
 LAST_CUTS = [256,256,256,256]
-SPLIT = 256
+SPLIT = 128
 ID_CUTS = [256,128,128]
 
 
@@ -52,10 +52,11 @@ def tile_picked_hash_lin_silu_sub_l_kernel(tc, xT, w_words, w_scales, b, offs, o
         raw0 = load("raw0", planes[:, 0, :], [P, T])
         nc.sync.dma_start(offsets[:], offs)
         raw23 = pool.tile([P, 2, T], F32, name="raw23")
-        nc.sync.dma_start(raw23[:, 0, :], planes[:, 2, :])
         for a, z in spans(PAIR_CUTS):
-            nc.sync.dma_start(raw23[:, 1, a:z], planes[:, 3, a:z])
-        raw1 = [load("raw1_%d" % a, planes[:, 1, a:z], [P, z - a]) for a, z in spans(LAST_CUTS)]
+            nc.sync.dma_start(raw23[:, :, a:z], planes[:, 2:4, a:z])
+        raw1 = pool.tile([P, T], F32, name="raw1")
+        for a, z in spans(LAST_CUTS):
+            nc.sync.dma_start(raw1[:, a:z], planes[:, 1, a:z])
 
         w_codes = pool.tile([P, N], U32, name="w_codes", align_bytes=64)
         nc.sync.dma_start(w_codes[:].bitcast(I32), w_words[0].rearrange("p n r -> p (n r)").bitcast(I32))
@@ -92,15 +93,18 @@ def tile_picked_hash_lin_silu_sub_l_kernel(tc, xT, w_words, w_scales, b, offs, o
 
         def cast_last(i, copy):
             a, z = spans(LAST_CUTS)[i]
-            copy(win1[:, a:z], raw1[i][:])
+            copy(win1[:, a:z], raw1[:, a:z])
 
         for i in range(len(LAST_CUTS)):
             cast_last(i, nc.scalar.copy)
         for d in range(D):
             gather_words(d, 0, V)
+        last_ids = spans(ID_CUTS)[-1]
+        nc.vector.tensor_copy(half_words(1, 1, *last_ids), raw1[:].indirect(list_slice(1, *last_ids)))
         for a, z in spans(ID_CUTS):
             for d in range(D):
-                gather_half(win1, 1, d, a, z)
+                if (d, (a, z)) != (1, last_ids):
+                    gather_half(win1, 1, d, a, z)
 
         sums = [pool.tile([P, 4 * w], BF16, name="sum_%d" % c, align_bytes=64) for c, w in enumerate(ID_CUTS)]
 

@@ -16,11 +16,10 @@ ACT = mybir.ActivationFunctionType
 ADD = mybir.AluOpType.add
 
 P = 128
-FIRST_CUTS = [640,384]
-PAIR_CUTS = [512,256,256]
-LAST_CUTS = [256,256,256,256]
-SPLIT = 128
-ID_CUTS = [256,128,128]
+PAIR_CUTS = [512, 256, 256]
+LAST_CUTS = [384, 384, 256]
+SPLIT = 384
+ID_CUTS = [256, 128, 128]
 
 
 def spans(widths):
@@ -44,19 +43,17 @@ def tile_picked_hash_lin_silu_sub_l_kernel(tc, xT, w_words, w_scales, b, offs, o
         nc.vector.memset(w_scale[:].bitcast(I32), 0)
         nc.scalar.activation(warm_out[:], warm_in[:], ACT.Silu)
 
-        def load(name, src, shape):
-            raw = pool.tile(shape, F32, name=name)
-            nc.sync.dma_start(raw[:], src)
-            return raw
-
-        raw0 = load("raw0", planes[:, 0, :], [P, T])
-        nc.sync.dma_start(offsets[:], offs)
-        raw23 = pool.tile([P, 2, T], F32, name="raw23")
-        for a, z in spans(PAIR_CUTS):
-            nc.sync.dma_start(raw23[:, :, a:z], planes[:, 2:4, a:z])
         raw1 = pool.tile([P, T], F32, name="raw1")
+        nc.sync.dma_start(raw1[:], planes[:, 1, :])
+        nc.sync.dma_start(offsets[:], offs)
+        raw3 = pool.tile([P, T], F32, name="raw3")
+        nc.sync.dma_start(raw3[:], planes[:, 3, :])
+        raw2 = [pool.tile([P, w], F32, name="raw2_%d" % i) for i, w in enumerate(PAIR_CUTS)]
+        for piece, (a, z) in zip(raw2, spans(PAIR_CUTS)):
+            nc.sync.dma_start(piece[:], planes[:, 2, a:z])
+        raw0 = pool.tile([P, T], F32, name="raw0")
         for a, z in spans(LAST_CUTS):
-            nc.sync.dma_start(raw1[:, a:z], planes[:, 1, a:z])
+            nc.sync.dma_start(raw0[:, a:z], planes[:, 0, a:z])
 
         w_codes = pool.tile([P, N], U32, name="w_codes", align_bytes=64)
         nc.sync.dma_start(w_codes[:].bitcast(I32), w_words[0].rearrange("p n r -> p (n r)").bitcast(I32))
@@ -65,9 +62,8 @@ def tile_picked_hash_lin_silu_sub_l_kernel(tc, xT, w_words, w_scales, b, offs, o
         bias = pool.tile([P, 1], F32, name="bias")
         nc.sync.dma_start(bias[:], b)
 
+        win1 = pool.tile([P, T], BF16, name="win1")
         win0 = pool.tile([P, T], BF16, name="win0")
-        win1 = raw0[:, 0 : T // 2].bitcast(BF16)
-        win23 = pool.tile([P, T], U32, name="win23")
         picked = pool.tile([P, D, 2, V], U32, name="picked")
 
         def list_slice(d, a, z):
@@ -79,32 +75,24 @@ def tile_picked_hash_lin_silu_sub_l_kernel(tc, xT, w_words, w_scales, b, offs, o
         def gather_half(window, e, d, a, z):
             nc.scalar.activation(half_words(e, d, a, z), window.indirect(list_slice(d, a, z)), ACT.Copy)
 
-        for copy, (a, z) in zip((nc.vector.tensor_copy, nc.scalar.copy), spans(FIRST_CUTS)):
-            copy(win0[:, a:z], raw0[:, a:z])
-        nc.vector.tensor_copy(half_words(0, 1, SPLIT, V), raw0[:].indirect(list_slice(1, SPLIT, V)))
-        for a, z in spans(PAIR_CUTS):
-            dst = win23[:, a:z].bitcast(BF16).rearrange("p (c e) -> p c e", e=2)
-            nc.vector.tensor_copy(dst, raw23[:, :, a:z].rearrange("p e c -> p c e"))
-        gather_half(win0[:], 0, 0, 0, V)
-        gather_half(win0[:], 0, 1, 0, SPLIT)
+        nc.scalar.copy(win1[:], raw1[:])
+        nc.vector.tensor_copy(picked[:, 1, 0, :].bitcast(F32), raw1[:].indirect(list_slice(1, 0, V)))
+        nc.vector.tensor_copy(picked[:, 0, 0, SPLIT:V].bitcast(F32), raw1[:].indirect(list_slice(0, SPLIT, V)))
+        gather_half(win1[:], 1, 0, 0, SPLIT)
+        for piece, (a, z) in zip(raw2, spans(PAIR_CUTS)):
+            low = raw3[:, a:z].bitcast(BF16).rearrange("p (c e) -> p c e", e=2)[:, :, 0]
+            nc.vector.tensor_copy(low, piece[:])
 
-        def gather_words(d, a, z):
-            nc.vector.tensor_copy(picked[:, d, 1, a:z], win23[:].indirect(list_slice(d, a, z)))
-
-        def cast_last(i, copy):
-            a, z = spans(LAST_CUTS)[i]
-            copy(win1[:, a:z], raw1[:, a:z])
-
-        for i in range(len(LAST_CUTS)):
-            cast_last(i, nc.scalar.copy)
+        for a, z in spans(LAST_CUTS):
+            nc.scalar.copy(win0[:, a:z], raw0[:, a:z])
         for d in range(D):
-            gather_words(d, 0, V)
+            nc.vector.tensor_copy(picked[:, d, 1, :], raw3[:].bitcast(U32).indirect(list_slice(d, 0, V)))
         last_ids = spans(ID_CUTS)[-1]
-        nc.vector.tensor_copy(half_words(1, 1, *last_ids), raw1[:].indirect(list_slice(1, *last_ids)))
+        nc.vector.tensor_copy(half_words(0, 1, *last_ids), raw0[:].indirect(list_slice(1, *last_ids)))
         for a, z in spans(ID_CUTS):
             for d in range(D):
                 if (d, (a, z)) != (1, last_ids):
-                    gather_half(win1, 1, d, a, z)
+                    gather_half(win0[:], 0, d, a, z)
 
         sums = [pool.tile([P, 4 * w], BF16, name="sum_%d" % c, align_bytes=64) for c, w in enumerate(ID_CUTS)]
 

@@ -16,7 +16,8 @@ ACT = mybir.ActivationFunctionType
 ADD = mybir.AluOpType.add
 
 P = 128
-PAIR_CUTS = [512, 256, 256]
+PAIR_CUTS = [384, 640]
+PAIR_CASTS = [128, 256, 640]
 LAST_CUTS = [384, 384, 256]
 SPLIT = 384
 ID_CUTS = [256, 128, 128]
@@ -46,11 +47,12 @@ def tile_picked_hash_lin_silu_sub_l_kernel(tc, xT, w_words, w_scales, b, offs, o
         raw1 = pool.tile([P, T], F32, name="raw1")
         nc.sync.dma_start(raw1[:], planes[:, 1, :])
         nc.sync.dma_start(offsets[:], offs)
-        raw3 = pool.tile([P, T], F32, name="raw3")
-        nc.sync.dma_start(raw3[:], planes[:, 3, :])
-        raw2 = [pool.tile([P, w], F32, name="raw2_%d" % i) for i, w in enumerate(PAIR_CUTS)]
-        for piece, (a, z) in zip(raw2, spans(PAIR_CUTS)):
-            nc.sync.dma_start(piece[:], planes[:, 2, a:z])
+        rows = xT.rearrange("(p t) c -> p (t c)", t=4)
+        raw23 = pool.tile([P, 2 * T], F32, name="raw23")
+        *late, (a, z) = spans(PAIR_CUTS)
+        nc.sync.dma_start(raw23[:, a : 2 * T], rows[:, 2 * T + a : 4 * T])
+        for a, z in reversed(late):
+            nc.sync.dma_start(raw23[:, a:z], rows[:, 2 * T + a : 2 * T + z])
         raw0 = pool.tile([P, T], F32, name="raw0")
         for a, z in spans(LAST_CUTS):
             nc.sync.dma_start(raw0[:, a:z], planes[:, 0, a:z])
@@ -79,14 +81,15 @@ def tile_picked_hash_lin_silu_sub_l_kernel(tc, xT, w_words, w_scales, b, offs, o
         nc.vector.tensor_copy(picked[:, 1, 0, :].bitcast(F32), raw1[:].indirect(list_slice(1, 0, V)))
         nc.vector.tensor_copy(picked[:, 0, 0, SPLIT:V].bitcast(F32), raw1[:].indirect(list_slice(0, SPLIT, V)))
         gather_half(win1[:], 1, 0, 0, SPLIT)
-        for piece, (a, z) in zip(raw2, spans(PAIR_CUTS)):
-            low = raw3[:, a:z].bitcast(BF16).rearrange("p (c e) -> p c e", e=2)[:, :, 0]
-            nc.vector.tensor_copy(low, piece[:])
+        copies = (nc.scalar.copy, nc.vector.tensor_copy, nc.vector.tensor_copy)
+        for copy, (a, z) in reversed(list(zip(copies, spans(PAIR_CASTS)))):
+            low = raw23[:, T + a : T + z].bitcast(BF16).rearrange("p (c e) -> p c e", e=2)[:, :, 0]
+            copy(low, raw23[:, a:z])
 
         for a, z in spans(LAST_CUTS):
             nc.scalar.copy(win0[:, a:z], raw0[:, a:z])
         for d in range(D):
-            nc.vector.tensor_copy(picked[:, d, 1, :], raw3[:].bitcast(U32).indirect(list_slice(d, 0, V)))
+            nc.vector.tensor_copy(picked[:, d, 1, :], raw23[:, T : 2 * T].bitcast(U32).indirect(list_slice(d, 0, V)))
         last_ids = spans(ID_CUTS)[-1]
         nc.vector.tensor_copy(half_words(0, 1, *last_ids), raw0[:].indirect(list_slice(1, *last_ids)))
         for a, z in spans(ID_CUTS):

@@ -14,12 +14,11 @@ U8 = mybir.dt.uint8
 FP8X4 = mybir.dt.float8_e4m3fn_x4
 ACT = mybir.ActivationFunctionType
 ADD = mybir.AluOpType.add
+MULT = mybir.AluOpType.mult
 
 P = 128
-PAIR_CUTS = [384, 640]
-PAIR_CASTS = [128, 256, 640]
-LAST_CUTS = [384, 384, 256]
-SPLIT = 384
+ORDER = [1, 0, 3, 2]
+SPLIT = 256
 ID_CUTS = [256, 128, 128]
 
 
@@ -44,18 +43,12 @@ def tile_picked_hash_lin_silu_sub_l_kernel(tc, xT, w_words, w_scales, b, offs, o
         nc.vector.memset(w_scale[:].bitcast(I32), 0)
         nc.scalar.activation(warm_out[:], warm_in[:], ACT.Silu)
 
-        raw1 = pool.tile([P, T], F32, name="raw1")
-        nc.sync.dma_start(raw1[:], planes[:, 1, :])
+        raw = {t: pool.tile([P, T], F32, name="raw%d" % t) for t in ORDER}
+        win = {t: pool.tile([P, T], BF16, name="win%d" % t) for t in ORDER}
+        nc.sync.dma_start(raw[ORDER[0]][:], planes[:, ORDER[0], :])
         nc.sync.dma_start(offsets[:], offs)
-        rows = xT.rearrange("(p t) c -> p (t c)", t=4)
-        raw23 = pool.tile([P, 2 * T], F32, name="raw23")
-        *late, (a, z) = spans(PAIR_CUTS)
-        nc.sync.dma_start(raw23[:, a : 2 * T], rows[:, 2 * T + a : 4 * T])
-        for a, z in reversed(late):
-            nc.sync.dma_start(raw23[:, a:z], rows[:, 2 * T + a : 2 * T + z])
-        raw0 = pool.tile([P, T], F32, name="raw0")
-        for a, z in spans(LAST_CUTS):
-            nc.sync.dma_start(raw0[:, a:z], planes[:, 0, a:z])
+        for t in ORDER[1:]:
+            nc.sync.dma_start(raw[t][:], planes[:, t, :])
 
         w_codes = pool.tile([P, N], U32, name="w_codes", align_bytes=64)
         nc.sync.dma_start(w_codes[:].bitcast(I32), w_words[0].rearrange("p n r -> p (n r)").bitcast(I32))
@@ -64,40 +57,28 @@ def tile_picked_hash_lin_silu_sub_l_kernel(tc, xT, w_words, w_scales, b, offs, o
         bias = pool.tile([P, 1], F32, name="bias")
         nc.sync.dma_start(bias[:], b)
 
-        win1 = pool.tile([P, T], BF16, name="win1")
-        win0 = pool.tile([P, T], BF16, name="win0")
         picked = pool.tile([P, D, 2, V], U32, name="picked")
 
         def list_slice(d, a, z):
             return offsets[:, (d * V + a) // 16 : (d * V + z) // 16]
 
-        def half_words(e, d, a, z):
-            return picked[:, d, 0, a:z].bitcast(BF16).rearrange("p (v e) -> p v e", e=2)[:, :, e]
+        def half_words(t, d, a, z):
+            return picked[:, d, t // 2, a:z].bitcast(BF16).rearrange("p (v e) -> p v e", e=2)[:, :, t % 2]
 
-        def gather_half(window, e, d, a, z):
-            nc.scalar.activation(half_words(e, d, a, z), window.indirect(list_slice(d, a, z)), ACT.Copy)
-
-        nc.scalar.copy(win1[:], raw1[:])
-        nc.vector.tensor_copy(picked[:, 1, 0, :].bitcast(F32), raw1[:].indirect(list_slice(1, 0, V)))
-        nc.vector.tensor_copy(picked[:, 0, 0, SPLIT:V].bitcast(F32), raw1[:].indirect(list_slice(0, SPLIT, V)))
-        gather_half(win1[:], 1, 0, 0, SPLIT)
-        copies = (nc.scalar.copy, nc.vector.tensor_copy, nc.vector.tensor_copy)
-        for copy, (a, z) in reversed(list(zip(copies, spans(PAIR_CASTS)))):
-            low = raw23[:, T + a : T + z].bitcast(BF16).rearrange("p (c e) -> p c e", e=2)[:, :, 0]
-            copy(low, raw23[:, a:z])
-
-        for a, z in spans(LAST_CUTS):
-            nc.scalar.copy(win0[:, a:z], raw0[:, a:z])
-        for d in range(D):
-            nc.vector.tensor_copy(picked[:, d, 1, :], raw23[:, T : 2 * T].bitcast(U32).indirect(list_slice(d, 0, V)))
-        last_ids = spans(ID_CUTS)[-1]
-        nc.vector.tensor_copy(half_words(0, 1, *last_ids), raw0[:].indirect(list_slice(1, *last_ids)))
-        for a, z in spans(ID_CUTS):
+        for t in ORDER:
+            if t == ORDER[0]:
+                nc.scalar.copy(win[t][:], raw[t][:])
+            else:
+                nc.gpsimd.tensor_scalar(win[t][:], raw[t][:], 1.0, 0.0, MULT, ADD)
             for d in range(D):
-                if (d, (a, z)) != (1, last_ids):
-                    gather_half(win0[:], 0, d, a, z)
+                target = picked[:, d, t // 2, 0:SPLIT].bitcast(F32) if t % 2 else half_words(t, d, 0, SPLIT)
+                nc.vector.tensor_copy(target, raw[t][:].indirect(list_slice(d, 0, SPLIT)))
+            for a, z in spans(ID_CUTS)[1:] if t == ORDER[-1] else [(SPLIT, V)]:
+                for d in range(D):
+                    nc.scalar.activation(half_words(t, d, a, z), win[t][:].indirect(list_slice(d, a, z)), ACT.Copy)
 
         sums = [pool.tile([P, 4 * w], BF16, name="sum_%d" % c, align_bytes=64) for c, w in enumerate(ID_CUTS)]
+        result = win[ORDER[-1]][:].bitcast(F32)
 
         def add(c):
             a, z = spans(ID_CUTS)[c]
@@ -114,12 +95,9 @@ def tile_picked_hash_lin_silu_sub_l_kernel(tc, xT, w_words, w_scales, b, offs, o
                 out=acc[:], lhsT=w_codes[:].bitcast(FP8X4), lhsT_scale=w_scale[:],
                 rhs=codes[:].bitcast(FP8X4), rhs_scale=scale[:], start=True, stop=True,
             )
-            result = pool.tile([P, z - a], F32, name="result_%d" % c)
-            nc.scalar.activation(result[:], acc[:], ACT.Silu, bias=bias[:])
-            nc.sync.dma_start(out[:, a:z], result[:])
+            nc.scalar.activation(result[:, a:z], acc[:], ACT.Silu, bias=bias[:])
+            nc.sync.dma_start(out[:, a:z], result[:, a:z])
 
-        add(0)
-        for c in range(1, len(ID_CUTS)):
+        for c in range(len(ID_CUTS)):
             add(c)
-            finish(c - 1)
-        finish(len(ID_CUTS) - 1)
+            finish(c)

@@ -19,7 +19,9 @@ MULT = mybir.AluOpType.mult
 P = 128
 ORDER = [1, 0, 3, 2]
 SPLIT = 256
-ID_CUTS = [256, 128, 128]
+FIRST_SPLIT = [256, 320]
+SCALAR_CAST = {1: T, 0: 0, 3: 0, 2: 0}
+ID_CUTS = [128, 128, 128, 128]
 
 
 def spans(widths):
@@ -66,18 +68,21 @@ def tile_picked_hash_lin_silu_sub_l_kernel(tc, xT, w_words, w_scales, b, offs, o
             return picked[:, d, t // 2, a:z].bitcast(BF16).rearrange("p (v e) -> p v e", e=2)[:, :, t % 2]
 
         for t in ORDER:
-            if t == ORDER[0]:
-                nc.scalar.copy(win[t][:], raw[t][:])
-            else:
-                nc.gpsimd.tensor_scalar(win[t][:], raw[t][:], 1.0, 0.0, MULT, ADD)
-            for d in range(D):
-                target = picked[:, d, t // 2, 0:SPLIT].bitcast(F32) if t % 2 else half_words(t, d, 0, SPLIT)
-                nc.vector.tensor_copy(target, raw[t][:].indirect(list_slice(d, 0, SPLIT)))
-            for a, z in spans(ID_CUTS)[1:] if t == ORDER[-1] else [(SPLIT, V)]:
-                for d in range(D):
-                    nc.scalar.activation(half_words(t, d, a, z), win[t][:].indirect(list_slice(d, a, z)), ACT.Copy)
+            cut = SCALAR_CAST[t]
+            if cut:
+                nc.scalar.copy(win[t][:, :cut], raw[t][:, :cut])
+            if cut < T:
+                nc.gpsimd.tensor_scalar(win[t][:, cut:], raw[t][:, cut:], 1.0, 0.0, MULT, ADD)
+            first = FIRST_SPLIT[t // 2]
+            chunks = spans(ID_CUTS)
+            last = t == ORDER[-1]
+            for d, a, z in [(0, 0, first)] + [(1, a, z) for a, z in (chunks[:2] if last else [(0, SPLIT)])]:
+                target = picked[:, d, t // 2, a:z].bitcast(F32) if t % 2 else half_words(t, d, a, z)
+                nc.vector.tensor_copy(target, raw[t][:].indirect(list_slice(d, a, z)))
+            for d, a, z in [(0, first, V)] + [(1, a, z) for a, z in (chunks[2:] if last else [(SPLIT, V)])]:
+                nc.scalar.activation(half_words(t, d, a, z), win[t][:].indirect(list_slice(d, a, z)), ACT.Copy)
 
-        sums = [pool.tile([P, 4 * w], BF16, name="sum_%d" % c, align_bytes=64) for c, w in enumerate(ID_CUTS)]
+        sums = [pool.tile([P, 4 * ID_CUTS[c]], BF16, name="sum_%d" % c, align_bytes=64) for c in range(2)] * 2
         result = win[ORDER[-1]][:].bitcast(F32)
 
         def add(c):
@@ -96,8 +101,16 @@ def tile_picked_hash_lin_silu_sub_l_kernel(tc, xT, w_words, w_scales, b, offs, o
                 rhs=codes[:].bitcast(FP8X4), rhs_scale=scale[:], start=True, stop=True,
             )
             nc.scalar.activation(result[:, a:z], acc[:], ACT.Silu, bias=bias[:])
+
+        def store(a, z):
             nc.sync.dma_start(out[:, a:z], result[:, a:z])
 
-        for c in range(len(ID_CUTS)):
+        add(0)
+        add(1)
+        finish(0)
+        finish(1)
+        store(0, SPLIT)
+        for c in (2, 3):
             add(c)
             finish(c)
+            store(*spans(ID_CUTS)[c])

@@ -17,16 +17,12 @@ ADD = mybir.AluOpType.add
 MULT = mybir.AluOpType.mult
 
 P = 128
-ORDER = [1, 0, 3, 2]
-SPLIT = 256
-FIRST_SPLIT = [256, 320]
-SCALAR_CAST = {1: T, 0: 0, 3: 0, 2: 0}
-ID_CUTS = [128, 128, 128, 128]
-
-
-def spans(widths):
-    starts = [sum(widths[:i]) for i in range(len(widths))]
-    return [(s, s + w) for s, w in zip(starts, widths)]
+S = D * V
+CHUNK = 128
+FIRST_CAST = 576
+FIRST_PIECE_SPLIT = 352
+VECTOR_SHARE_1 = 416
+VECTOR_SHARE_0 = 416
 
 
 def tile_picked_hash_lin_silu_sub_l_kernel(tc, xT, w_words, w_scales, b, offs, out):
@@ -36,7 +32,7 @@ def tile_picked_hash_lin_silu_sub_l_kernel(tc, xT, w_words, w_scales, b, offs, o
         psum = ctx.enter_context(tc.psum_pool(name="psum", bufs=1))
 
         planes = xT.rearrange("(p t) c -> p t c", t=4)
-        offsets = pool.tile([P, D * V // 16], U16, name="offsets")
+        offsets = pool.tile([P, S // 16], U16, name="offsets")
 
         warm_in = pool.tile([P, 1], F32, name="warm_in")
         warm_out = pool.tile([P, 1], F32, name="warm_out")
@@ -45,11 +41,10 @@ def tile_picked_hash_lin_silu_sub_l_kernel(tc, xT, w_words, w_scales, b, offs, o
         nc.vector.memset(w_scale[:].bitcast(I32), 0)
         nc.scalar.activation(warm_out[:], warm_in[:], ACT.Silu)
 
-        raw = {t: pool.tile([P, T], F32, name="raw%d" % t) for t in ORDER}
-        win = {t: pool.tile([P, T], BF16, name="win%d" % t) for t in ORDER}
-        nc.sync.dma_start(raw[ORDER[0]][:], planes[:, ORDER[0], :])
+        raw = [pool.tile([P, T], F32, name="raw%d" % t) for t in range(4)]
+        nc.sync.dma_start(raw[1][:], planes[:, 1, :])
         nc.sync.dma_start(offsets[:], offs)
-        for t in ORDER[1:]:
+        for t in (0, 3, 2):
             nc.sync.dma_start(raw[t][:], planes[:, t, :])
 
         w_codes = pool.tile([P, N], U32, name="w_codes", align_bytes=64)
@@ -59,43 +54,58 @@ def tile_picked_hash_lin_silu_sub_l_kernel(tc, xT, w_words, w_scales, b, offs, o
         bias = pool.tile([P, 1], F32, name="bias")
         nc.sync.dma_start(bias[:], b)
 
-        picked = pool.tile([P, D, 2, V], U32, name="picked")
+        picked = pool.tile([P, 2, S], U32, name="picked")
+        win = [pool.tile([P, T], BF16, name="win%d" % t) for t in range(4)]
 
-        def list_slice(d, a, z):
-            return offsets[:, (d * V + a) // 16 : (d * V + z) // 16]
+        def gpsimd_cast(t, cut):
+            nc.gpsimd.tensor_scalar(win[t][:, cut:], raw[t][:, cut:], 1.0, 0.0, MULT, ADD)
 
-        def half_words(t, d, a, z):
-            return picked[:, d, t // 2, a:z].bitcast(BF16).rearrange("p (v e) -> p v e", e=2)[:, :, t % 2]
+        def half_words(t, a, z):
+            return picked[:, t // 2, a:z].bitcast(BF16).rearrange("p (j e) -> p j e", e=2)[:, :, t % 2]
 
-        for t in ORDER:
-            cut = SCALAR_CAST[t]
-            if cut:
-                nc.scalar.copy(win[t][:, :cut], raw[t][:, :cut])
-            if cut < T:
-                nc.gpsimd.tensor_scalar(win[t][:, cut:], raw[t][:, cut:], 1.0, 0.0, MULT, ADD)
-            first = FIRST_SPLIT[t // 2]
-            chunks = spans(ID_CUTS)
-            last = t == ORDER[-1]
-            for d, a, z in [(0, 0, first)] + [(1, a, z) for a, z in (chunks[:2] if last else [(0, SPLIT)])]:
-                target = picked[:, d, t // 2, a:z].bitcast(F32) if t % 2 else half_words(t, d, a, z)
-                nc.vector.tensor_copy(target, raw[t][:].indirect(list_slice(d, a, z)))
-            for d, a, z in [(0, first, V)] + [(1, a, z) for a, z in (chunks[2:] if last else [(SPLIT, V)])]:
-                nc.scalar.activation(half_words(t, d, a, z), win[t][:].indirect(list_slice(d, a, z)), ACT.Copy)
+        def vector_gather(t, a, z):
+            target = picked[:, t // 2, a:z].bitcast(F32) if t % 2 else half_words(t, a, z)
+            nc.vector.tensor_copy(target, raw[t][:].indirect(offsets[:, a // 16 : z // 16]))
 
-        sums = [pool.tile([P, 4 * ID_CUTS[c]], BF16, name="sum_%d" % c, align_bytes=64) for c in range(2)] * 2
-        result = win[ORDER[-1]][:].bitcast(F32)
+        def scalar_gather(t, a, z):
+            nc.scalar.activation(half_words(t, a, z), win[t][:].indirect(offsets[:, a // 16 : z // 16]), ACT.Copy)
+
+        nc.scalar.copy(win[1][:, :FIRST_CAST], raw[1][:, :FIRST_CAST])
+        gpsimd_cast(1, FIRST_CAST)
+        vector_gather(1, 0, VECTOR_SHARE_1)
+        scalar_gather(1, VECTOR_SHARE_1, S)
+        gpsimd_cast(0, 0)
+        vector_gather(0, 0, VECTOR_SHARE_0)
+        scalar_gather(0, VECTOR_SHARE_0, S)
+        gpsimd_cast(3, 0)
+        vector_gather(3, 0, FIRST_PIECE_SPLIT)
+        vector_gather(3, V, V + 2 * CHUNK)
+        scalar_gather(3, FIRST_PIECE_SPLIT, V)
+        scalar_gather(3, V + 2 * CHUNK, S)
+        gpsimd_cast(2, 0)
+        vector_gather(2, 0, FIRST_PIECE_SPLIT)
+        for c in range(2):
+            vector_gather(2, V + c * CHUNK, V + (c + 1) * CHUNK)
+        scalar_gather(2, FIRST_PIECE_SPLIT, V)
+        for c in range(2, 4):
+            scalar_gather(2, V + c * CHUNK, V + (c + 1) * CHUNK)
+
+        sums = [pool.tile([P, 4 * CHUNK], BF16, name="sum_%d" % c, align_bytes=64) for c in range(2)] * 2
+        result = win[2][:].bitcast(F32)
 
         def add(c):
-            a, z = spans(ID_CUTS)[c]
-            rows = [picked[:, d, :, a:z].bitcast(BF16).rearrange("p u (v e) -> p v u e", e=2) for d in range(D)]
+            a, z = c * CHUNK, (c + 1) * CHUNK
+            rows = [
+                picked[:, :, d * V + a : d * V + z].bitcast(BF16).rearrange("p u (v e) -> p v u e", e=2) for d in range(D)
+            ]
             nc.vector.tensor_tensor(sums[c][:].rearrange("p (v u e) -> p v u e", u=2, e=2), rows[0], rows[1], ADD)
 
         def finish(c):
-            a, z = spans(ID_CUTS)[c]
-            codes = pool.tile([P, z - a], U32, name="codes_%d" % c, align_bytes=64)
-            scale = pool.tile([P, z - a], U8, name="scale_%d" % c, align_bytes=64)
+            a, z = c * CHUNK, (c + 1) * CHUNK
+            codes = pool.tile([P, CHUNK], U32, name="codes_%d" % c, align_bytes=64)
+            scale = pool.tile([P, CHUNK], U8, name="scale_%d" % c, align_bytes=64)
             nc.vector.quantize_mx(out=codes[:].bitcast(FP8X4), scales=scale[:], in_=sums[c][:])
-            acc = psum.tile([P, z - a], F32, name="acc_%d" % c)
+            acc = psum.tile([P, CHUNK], F32, name="acc_%d" % c)
             nc.tensor.matmul_mx(
                 out=acc[:], lhsT=w_codes[:].bitcast(FP8X4), lhsT_scale=w_scale[:],
                 rhs=codes[:].bitcast(FP8X4), rhs_scale=scale[:], start=True, stop=True,
@@ -109,8 +119,9 @@ def tile_picked_hash_lin_silu_sub_l_kernel(tc, xT, w_words, w_scales, b, offs, o
         add(1)
         finish(0)
         finish(1)
-        store(0, SPLIT)
+        store(0, 2 * CHUNK)
+        add(2)
+        add(3)
         for c in (2, 3):
-            add(c)
             finish(c)
-            store(*spans(ID_CUTS)[c])
+            store(c * CHUNK, (c + 1) * CHUNK)

@@ -22,7 +22,7 @@ CHUNK = 128
 FIRST_CAST = 576
 FIRST_PIECE_SPLIT = 352
 VECTOR_SHARE_1 = 416
-VECTOR_SHARE_0 = 416
+VECTOR_SHARE_0 = 352
 
 
 def tile_picked_hash_lin_silu_sub_l_kernel(tc, xT, w_words, w_scales, b, offs, out):

@@ -19,10 +19,7 @@ MULT = mybir.AluOpType.mult
 P = 128
 S = D * V
 CHUNK = 128
-FIRST_CAST = 576
-FIRST_PIECE_SPLIT = 352
-VECTOR_SHARE_1 = 416
-VECTOR_SHARE_0 = 352
+VECTOR_SHARE_1 = 448
 
 
 def tile_picked_hash_lin_silu_sub_l_kernel(tc, xT, w_words, w_scales, b, offs, out):
@@ -55,43 +52,31 @@ def tile_picked_hash_lin_silu_sub_l_kernel(tc, xT, w_words, w_scales, b, offs, o
         nc.sync.dma_start(bias[:], b)
 
         picked = pool.tile([P, 2, S], U32, name="picked")
-        win = [pool.tile([P, T], BF16, name="win%d" % t) for t in range(4)]
+        window = pool.tile([P, T], BF16, name="window")
 
-        def gpsimd_cast(t, cut):
-            nc.gpsimd.tensor_scalar(win[t][:, cut:], raw[t][:, cut:], 1.0, 0.0, MULT, ADD)
+        def picks(a, z):
+            return offsets[:, a // 16 : z // 16]
 
-        def half_words(t, a, z):
-            return picked[:, t // 2, a:z].bitcast(BF16).rearrange("p (j e) -> p j e", e=2)[:, :, t % 2]
+        def whole_words(t, a, z):
+            return picked[:, t // 2, a:z].bitcast(F32)
 
-        def vector_gather(t, a, z):
-            target = picked[:, t // 2, a:z].bitcast(F32) if t % 2 else half_words(t, a, z)
-            nc.vector.tensor_copy(target, raw[t][:].indirect(offsets[:, a // 16 : z // 16]))
+        def low_halves(t, a, z):
+            return picked[:, t // 2, a:z].bitcast(BF16).rearrange("p (j e) -> p j e", e=2)[:, :, 0]
 
-        def scalar_gather(t, a, z):
-            nc.scalar.activation(half_words(t, a, z), win[t][:].indirect(offsets[:, a // 16 : z // 16]), ACT.Copy)
-
-        nc.scalar.copy(win[1][:, :FIRST_CAST], raw[1][:, :FIRST_CAST])
-        gpsimd_cast(1, FIRST_CAST)
-        vector_gather(1, 0, VECTOR_SHARE_1)
-        scalar_gather(1, VECTOR_SHARE_1, S)
-        gpsimd_cast(0, 0)
-        vector_gather(0, 0, VECTOR_SHARE_0)
-        scalar_gather(0, VECTOR_SHARE_0, S)
-        gpsimd_cast(3, 0)
-        vector_gather(3, 0, FIRST_PIECE_SPLIT)
-        vector_gather(3, V, V + 2 * CHUNK)
-        scalar_gather(3, FIRST_PIECE_SPLIT, V)
-        scalar_gather(3, V + 2 * CHUNK, S)
-        gpsimd_cast(2, 0)
-        vector_gather(2, 0, FIRST_PIECE_SPLIT)
-        for c in range(2):
-            vector_gather(2, V + c * CHUNK, V + (c + 1) * CHUNK)
-        scalar_gather(2, FIRST_PIECE_SPLIT, V)
-        for c in range(2, 4):
-            scalar_gather(2, V + c * CHUNK, V + (c + 1) * CHUNK)
+        nc.vector.tensor_copy(whole_words(1, 0, VECTOR_SHARE_1), raw[1][:].indirect(picks(0, VECTOR_SHARE_1)))
+        nc.scalar.activation(whole_words(1, VECTOR_SHARE_1, S), raw[1][:].indirect(picks(VECTOR_SHARE_1, S)), ACT.Copy)
+        for a, z in ((0, VECTOR_SHARE_1), (VECTOR_SHARE_1, S)):
+            nc.vector.tensor_copy(low_halves(0, a, z), raw[0][:].indirect(picks(a, z)))
+        for a, z in ((0, 2 * CHUNK), (V, V + 2 * CHUNK), (2 * CHUNK, V), (V + 2 * CHUNK, S)):
+            nc.scalar.activation(whole_words(3, a, z), raw[3][:].indirect(picks(a, z)), ACT.Copy)
+        nc.gpsimd.tensor_scalar(window[:], raw[2][:], 1.0, 0.0, MULT, ADD)
+        for a, z in ((0, 2 * CHUNK), (V, V + CHUNK), (V + CHUNK, V + 2 * CHUNK)):
+            nc.vector.tensor_copy(low_halves(2, a, z), raw[2][:].indirect(picks(a, z)))
+        for a, z in ((2 * CHUNK, V), (V + 2 * CHUNK, V + 3 * CHUNK), (V + 3 * CHUNK, S)):
+            nc.scalar.activation(low_halves(2, a, z), window[:].indirect(picks(a, z)), ACT.Copy)
 
         sums = [pool.tile([P, 4 * CHUNK], BF16, name="sum_%d" % c, align_bytes=64) for c in range(2)] * 2
-        result = win[2][:].bitcast(F32)
+        result = window[:].bitcast(F32)
 
         def add(c):
             a, z = c * CHUNK, (c + 1) * CHUNK

@@ -14,12 +14,12 @@ U8 = mybir.dt.uint8
 FP8X4 = mybir.dt.float8_e4m3fn_x4
 ACT = mybir.ActivationFunctionType
 ADD = mybir.AluOpType.add
-MULT = mybir.AluOpType.mult
 
 P = 128
 S = D * V
 CHUNK = 128
-VECTOR_SHARE_1 = 448
+HALF = V // 2
+VECTOR_IDS = 3 * CHUNK
 
 
 def tile_picked_hash_lin_silu_sub_l_kernel(tc, xT, w_words, w_scales, b, offs, out):
@@ -39,9 +39,9 @@ def tile_picked_hash_lin_silu_sub_l_kernel(tc, xT, w_words, w_scales, b, offs, o
         nc.scalar.activation(warm_out[:], warm_in[:], ACT.Silu)
 
         raw = [pool.tile([P, T], F32, name="raw%d" % t) for t in range(4)]
-        nc.sync.dma_start(raw[1][:], planes[:, 1, :])
+        nc.sync.dma_start(raw[0][:], planes[:, 0, :])
         nc.sync.dma_start(offsets[:], offs)
-        for t in (0, 3, 2):
+        for t in (2, 1, 3):
             nc.sync.dma_start(raw[t][:], planes[:, t, :])
 
         w_codes = pool.tile([P, N], U32, name="w_codes", align_bytes=64)
@@ -51,39 +51,69 @@ def tile_picked_hash_lin_silu_sub_l_kernel(tc, xT, w_words, w_scales, b, offs, o
         bias = pool.tile([P, 1], F32, name="bias")
         nc.sync.dma_start(bias[:], b)
 
-        picked = pool.tile([P, 2, S], U32, name="picked")
-        window = pool.tile([P, T], BF16, name="window")
+        picked = pool.tile([P, 2 * S + CHUNK], U32, name="picked")
+        spare = 2 * S
 
-        def picks(a, z):
-            return offsets[:, a // 16 : z // 16]
+        def looked_up(t, a, z):
+            return raw[t][:].indirect(offsets[:, a // 16 : z // 16])
 
-        def whole_words(t, a, z):
-            return picked[:, t // 2, a:z].bitcast(F32)
+        def place(t, a):
+            return t // 2 * S + a
 
-        def low_halves(t, a, z):
-            return picked[:, t // 2, a:z].bitcast(BF16).rearrange("p (j e) -> p j e", e=2)[:, :, 0]
+        def whole_words(at, n):
+            return picked[:, at : at + n].bitcast(F32)
 
-        nc.vector.tensor_copy(whole_words(1, 0, VECTOR_SHARE_1), raw[1][:].indirect(picks(0, VECTOR_SHARE_1)))
-        nc.scalar.activation(whole_words(1, VECTOR_SHARE_1, S), raw[1][:].indirect(picks(VECTOR_SHARE_1, S)), ACT.Copy)
-        for a, z in ((0, VECTOR_SHARE_1), (VECTOR_SHARE_1, S)):
-            nc.vector.tensor_copy(low_halves(0, a, z), raw[0][:].indirect(picks(a, z)))
-        for a, z in ((0, 2 * CHUNK), (V, V + 2 * CHUNK), (2 * CHUNK, V), (V + 2 * CHUNK, S)):
-            nc.scalar.activation(whole_words(3, a, z), raw[3][:].indirect(picks(a, z)), ACT.Copy)
-        nc.gpsimd.tensor_scalar(window[:], raw[2][:], 1.0, 0.0, MULT, ADD)
-        for a, z in ((0, 2 * CHUNK), (V, V + CHUNK), (V + CHUNK, V + 2 * CHUNK)):
-            nc.vector.tensor_copy(low_halves(2, a, z), raw[2][:].indirect(picks(a, z)))
-        for a, z in ((2 * CHUNK, V), (V + 2 * CHUNK, V + 3 * CHUNK), (V + 3 * CHUNK, S)):
-            nc.scalar.activation(low_halves(2, a, z), window[:].indirect(picks(a, z)), ACT.Copy)
+        def halves(at, n, e):
+            return picked[:, at : at + n].bitcast(BF16).rearrange("p (j e) -> p j e", e=2)[:, :, e]
+
+        def vector_words(t, a, z):
+            nc.vector.tensor_copy(whole_words(place(t, a), z - a), looked_up(t, a, z))
+
+        def vector_high_halves(t, a, z):
+            nc.vector.tensor_copy(halves(place(t, a), z - a, 1), looked_up(t, a, z))
+
+        def scalar_words(t, a, z, at=None):
+            nc.scalar.activation(whole_words(place(t, a) if at is None else at, z - a), looked_up(t, a, z), ACT.Copy)
+
+        loose = pool.tile([P, 2, V], BF16, name="loose")
+
+        def scalar_loose(t, a, z):
+            nc.scalar.activation(loose[:, t // 2, a:z], looked_up(t, V + a, V + z), ACT.Copy)
+
+        def sum_even_plane(t, a, z, at=None):
+            low = halves(place(t, a) if at is None else at, z - a, 0)
+            nc.gpsimd.tensor_tensor(low, halves(place(t, a), z - a, 1), loose[:, t // 2, a:z], ADD)
+
+        for a in (0, HALF):
+            vector_words(0, a, a + HALF)
+            scalar_loose(0, a, a + HALF)
+            sum_even_plane(0, a, a + HALF)
+        vector_words(2, 0, V)
+        scalar_loose(2, 0, V)
+        sum_even_plane(2, 0, VECTOR_IDS)
+        vector_high_halves(1, 0, V)
+        scalar_words(1, V, S)
+        vector_high_halves(3, 0, VECTOR_IDS)
+        scalar_words(3, VECTOR_IDS, V, spare)
+        sum_even_plane(2, VECTOR_IDS, V, spare)
+        scalar_words(3, V, V + HALF)
+        scalar_words(3, V + HALF, V + VECTOR_IDS)
+        scalar_words(3, V + VECTOR_IDS, S)
 
         sums = [pool.tile([P, 4 * CHUNK], BF16, name="sum_%d" % c, align_bytes=64) for c in range(2)] * 2
-        result = window[:].bitcast(F32)
+        result = pool.tile([P, V], F32, name="result")
+
+        chunks = picked[:].rearrange("p (r v) -> p r v", v=CHUNK)
+
+        def word_pairs(low, high):
+            rows = chunks[:, low // CHUNK : high // CHUNK + 1 : (high - low) // CHUNK, :]
+            return rows.bitcast(BF16).rearrange("p u (v e) -> p v u e", e=2)
 
         def add(c):
-            a, z = c * CHUNK, (c + 1) * CHUNK
-            rows = [
-                picked[:, :, d * V + a : d * V + z].bitcast(BF16).rearrange("p u (v e) -> p v u e", e=2) for d in range(D)
-            ]
-            nc.vector.tensor_tensor(sums[c][:].rearrange("p (v u e) -> p v u e", u=2, e=2), rows[0], rows[1], ADD)
+            a = c * CHUNK
+            first = word_pairs(place(1, a), place(3, a) if a < VECTOR_IDS else spare)
+            second = word_pairs(place(1, V + a), place(3, V + a))
+            nc.vector.tensor_tensor(sums[c][:].rearrange("p (v u e) -> p v u e", u=2, e=2), first, second, ADD)
 
         def finish(c):
             a, z = c * CHUNK, (c + 1) * CHUNK

@@ -19,7 +19,8 @@ P = 128
 S = D * V
 CHUNK = 128
 HALF = V // 2
-VECTOR_IDS = 3 * CHUNK
+VECTOR_SHARE_2 = 384
+PARKED_AT = 192
 
 
 def tile_picked_hash_lin_silu_sub_l_kernel(tc, xT, w_words, w_scales, b, offs, out):
@@ -51,91 +52,86 @@ def tile_picked_hash_lin_silu_sub_l_kernel(tc, xT, w_words, w_scales, b, offs, o
         bias = pool.tile([P, 1], F32, name="bias")
         nc.sync.dma_start(bias[:], b)
 
-        picked = pool.tile([P, 2 * S + CHUNK], U32, name="picked")
-        spare = 2 * S
+        first = pool.tile([P, 2, S], U32, name="first")
+        second = [pool.tile([P, 2, HALF], U32, name="second%d" % h) for h in range(2)]
 
         def looked_up(t, a, z):
             return raw[t][:].indirect(offsets[:, a // 16 : z // 16])
 
-        def place(t, a):
-            return t // 2 * S + a
-
-        def whole_words(at, n):
-            return picked[:, at : at + n].bitcast(F32)
-
-        def halves(at, n, e):
-            return picked[:, at : at + n].bitcast(BF16).rearrange("p (j e) -> p j e", e=2)[:, :, e]
+        def halves(t, a, z, e):
+            return first[:, t // 2, a:z].bitcast(BF16).rearrange("p (j e) -> p j e", e=2)[:, :, e]
 
         def vector_words(t, a, z):
-            nc.vector.tensor_copy(whole_words(place(t, a), z - a), looked_up(t, a, z))
+            nc.vector.tensor_copy(first[:, t // 2, a:z].bitcast(F32), looked_up(t, a, z))
+
+        def scalar_words(t, a, z):
+            nc.scalar.activation(first[:, t // 2, a:z].bitcast(F32), looked_up(t, a, z), ACT.Copy)
+
+        def high_halves(words):
+            return words.bitcast(BF16).rearrange("p (j e) -> p j e", e=2)[:, :, 1]
+
+        def sum_even_plane(t, a, z, other):
+            nc.gpsimd.tensor_tensor(halves(t, a, z, 0), halves(t, a, z, 1), high_halves(other), ADD)
 
         def vector_high_halves(t, a, z):
-            nc.vector.tensor_copy(halves(place(t, a), z - a, 1), looked_up(t, a, z))
+            nc.vector.tensor_copy(halves(t, a, z, 1), looked_up(t, a, z))
 
-        def scalar_words(t, a, z, at=None):
-            nc.scalar.activation(whole_words(place(t, a) if at is None else at, z - a), looked_up(t, a, z), ACT.Copy)
-
-        loose = pool.tile([P, 2, V], BF16, name="loose")
-
-        def scalar_loose(t, a, z):
-            nc.scalar.activation(loose[:, t // 2, a:z], looked_up(t, V + a, V + z), ACT.Copy)
-
-        def sum_even_plane(t, a, z, at=None):
-            low = halves(place(t, a) if at is None else at, z - a, 0)
-            nc.gpsimd.tensor_tensor(low, halves(place(t, a), z - a, 1), loose[:, t // 2, a:z], ADD)
+        def scalar_second_piece(t, a, z):
+            target = second[a // HALF][:, t // 2, a % HALF : a % HALF + z - a]
+            nc.scalar.activation(target.bitcast(F32), looked_up(t, V + a, V + z), ACT.Copy)
 
         for a in (0, HALF):
             vector_words(0, a, a + HALF)
-            scalar_loose(0, a, a + HALF)
-            sum_even_plane(0, a, a + HALF)
-        vector_words(2, 0, V)
-        scalar_loose(2, 0, V)
-        sum_even_plane(2, 0, VECTOR_IDS)
-        vector_high_halves(1, 0, V)
-        scalar_words(1, V, S)
-        vector_high_halves(3, 0, VECTOR_IDS)
-        scalar_words(3, VECTOR_IDS, V, spare)
-        sum_even_plane(2, VECTOR_IDS, V, spare)
-        scalar_words(3, V, V + HALF)
-        scalar_words(3, V + HALF, V + VECTOR_IDS)
-        scalar_words(3, V + VECTOR_IDS, S)
+            scalar_words(0, V + a, V + a + HALF)
+            sum_even_plane(0, a, a + HALF, first[:, 0, V + a : V + a + HALF])
 
-        sums = [pool.tile([P, 4 * CHUNK], BF16, name="sum_%d" % c, align_bytes=64) for c in range(2)] * 2
-        result = pool.tile([P, V], F32, name="result")
+        vector_words(2, 0, VECTOR_SHARE_2)
+        scalar_words(2, VECTOR_SHARE_2, V + HALF)
+        sum_even_plane(2, 0, HALF, first[:, 1, V : V + HALF])
+        parked = second[1][:].rearrange("p u v -> p (u v)")[:, PARKED_AT : PARKED_AT + HALF]
+        nc.scalar.activation(parked.bitcast(F32), looked_up(2, V + HALF, S), ACT.Copy)
+        sum_even_plane(2, HALF, V, parked)
 
-        chunks = picked[:].rearrange("p (r v) -> p r v", v=CHUNK)
+        for t in (1, 3):
+            for a in (0, HALF):
+                vector_high_halves(t, a, a + HALF)
+        for t, a, z in ((1, 0, HALF), (3, 0, HALF), (1, HALF, V), (3, HALF, 3 * CHUNK), (3, 3 * CHUNK, V)):
+            scalar_second_piece(t, a, z)
 
-        def word_pairs(low, high):
-            rows = chunks[:, low // CHUNK : high // CHUNK + 1 : (high - low) // CHUNK, :]
-            return rows.bitcast(BF16).rearrange("p u (v e) -> p v u e", e=2)
+        sums = [pool.tile([P, 4 * CHUNK], BF16, name="sum_%d" % c, align_bytes=64) for c in range(4)]
+        codes = [pool.tile([P, CHUNK], U32, name="codes_%d" % c, align_bytes=64) for c in range(4)]
+        results = pool.tile([P, V], F32, name="results")
+
+        def result(a, z):
+            return results[:, a:z]
 
         def add(c):
-            a = c * CHUNK
-            first = word_pairs(place(1, a), place(3, a) if a < VECTOR_IDS else spare)
-            second = word_pairs(place(1, V + a), place(3, V + a))
-            nc.vector.tensor_tensor(sums[c][:].rearrange("p (v u e) -> p v u e", u=2, e=2), first, second, ADD)
+            a, z = c * CHUNK, (c + 1) * CHUNK
+            pieces = (first[:, :, a:z], second[a // HALF][:, :, a % HALF : a % HALF + CHUNK])
+            rows = [words.bitcast(BF16).rearrange("p u (c i e) -> p c u i e", i=2, e=2) for words in pieces]
+            nc.vector.tensor_tensor(sums[c][:].rearrange("p (i c u e) -> p c u i e", i=2, u=2, e=2), rows[0], rows[1], ADD)
 
         def finish(c):
             a, z = c * CHUNK, (c + 1) * CHUNK
-            codes = pool.tile([P, CHUNK], U32, name="codes_%d" % c, align_bytes=64)
             scale = pool.tile([P, CHUNK], U8, name="scale_%d" % c, align_bytes=64)
-            nc.vector.quantize_mx(out=codes[:].bitcast(FP8X4), scales=scale[:], in_=sums[c][:])
+            nc.vector.quantize_mx(out=codes[c][:].bitcast(FP8X4), scales=scale[:], in_=sums[c][:])
             acc = psum.tile([P, CHUNK], F32, name="acc_%d" % c)
             nc.tensor.matmul_mx(
                 out=acc[:], lhsT=w_codes[:].bitcast(FP8X4), lhsT_scale=w_scale[:],
-                rhs=codes[:].bitcast(FP8X4), rhs_scale=scale[:], start=True, stop=True,
+                rhs=codes[c][:].bitcast(FP8X4), rhs_scale=scale[:], start=True, stop=True,
             )
-            nc.scalar.activation(result[:, a:z], acc[:], ACT.Silu, bias=bias[:])
+            by_id = acc[:].rearrange("p (i c) -> p c i", i=2)
+            nc.scalar.activation(result(a, z).rearrange("p (c i) -> p c i", i=2), by_id, ACT.Silu, bias=bias[:])
 
         def store(a, z):
-            nc.sync.dma_start(out[:, a:z], result[:, a:z])
+            nc.sync.dma_start(out[:, a:z], result(a, z))
 
         add(0)
         add(1)
         finish(0)
-        finish(1)
-        store(0, 2 * CHUNK)
         add(2)
+        finish(1)
+        store(0, HALF)
         add(3)
         for c in (2, 3):
             finish(c)

@@ -19,8 +19,9 @@ P = 128
 S = D * V
 CHUNK = 128
 HALF = V // 2
-VECTOR_SHARE_2 = 384
-PARKED_AT = 192
+VECTOR_SHARE_1 = 384
+VECTOR_SHARE_0 = 512
+FIRST_CUT = 224
 
 
 def tile_picked_hash_lin_silu_sub_l_kernel(tc, xT, w_words, w_scales, b, offs, out):
@@ -40,9 +41,9 @@ def tile_picked_hash_lin_silu_sub_l_kernel(tc, xT, w_words, w_scales, b, offs, o
         nc.scalar.activation(warm_out[:], warm_in[:], ACT.Silu)
 
         raw = [pool.tile([P, T], F32, name="raw%d" % t) for t in range(4)]
-        nc.sync.dma_start(raw[0][:], planes[:, 0, :])
+        nc.sync.dma_start(raw[2][:], planes[:, 2, :])
         nc.sync.dma_start(offsets[:], offs)
-        for t in (2, 1, 3):
+        for t in (1, 0, 3):
             nc.sync.dma_start(raw[t][:], planes[:, t, :])
 
         w_codes = pool.tile([P, N], U32, name="w_codes", align_bytes=64)
@@ -52,51 +53,46 @@ def tile_picked_hash_lin_silu_sub_l_kernel(tc, xT, w_words, w_scales, b, offs, o
         bias = pool.tile([P, 1], F32, name="bias")
         nc.sync.dma_start(bias[:], b)
 
-        first = pool.tile([P, 2, S], U32, name="first")
-        second = [pool.tile([P, 2, HALF], U32, name="second%d" % h) for h in range(2)]
+        early = pool.tile([P, 12 * CHUNK], U32, name="early")
+        late = pool.tile([P, V], U32, name="late")
+        loose = pool.tile([P, S], BF16, name="loose")
+        low_first, low_second, high_second, high_first = 0, V, V + HALF, S
 
         def looked_up(t, a, z):
             return raw[t][:].indirect(offsets[:, a // 16 : z // 16])
 
-        def halves(t, a, z, e):
-            return first[:, t // 2, a:z].bitcast(BF16).rearrange("p (j e) -> p j e", e=2)[:, :, e]
+        def halves(words, e):
+            return words.bitcast(BF16).rearrange("p (j e) -> p j e", e=2)[:, :, e]
 
-        def vector_words(t, a, z):
-            nc.vector.tensor_copy(first[:, t // 2, a:z].bitcast(F32), looked_up(t, a, z))
+        def vector_gather(to, t, a, z):
+            nc.vector.tensor_copy(to, looked_up(t, a, z))
 
-        def scalar_words(t, a, z):
-            nc.scalar.activation(first[:, t // 2, a:z].bitcast(F32), looked_up(t, a, z), ACT.Copy)
+        def scalar_gather(to, t, a, z):
+            nc.scalar.activation(to, looked_up(t, a, z), ACT.Copy)
 
-        def high_halves(words):
-            return words.bitcast(BF16).rearrange("p (j e) -> p j e", e=2)[:, :, 1]
+        high_words = early[:, high_first : high_first + V]
+        vector_gather(high_words.bitcast(F32), 2, 0, V)
+        scalar_gather(late[:].bitcast(F32), 2, V, S)
+        nc.gpsimd.tensor_tensor(halves(high_words, 0), halves(high_words, 1), halves(late[:], 1), ADD)
 
-        def sum_even_plane(t, a, z, other):
-            nc.gpsimd.tensor_tensor(halves(t, a, z, 0), halves(t, a, z, 1), high_halves(other), ADD)
+        vector_gather(early[:, :VECTOR_SHARE_1].bitcast(F32), 1, 0, VECTOR_SHARE_1)
+        scalar_gather(early[:, VECTOR_SHARE_1 : V + HALF].bitcast(F32), 1, VECTOR_SHARE_1, V + HALF)
 
-        def vector_high_halves(t, a, z):
-            nc.vector.tensor_copy(halves(t, a, z, 1), looked_up(t, a, z))
-
-        def scalar_second_piece(t, a, z):
-            target = second[a // HALF][:, t // 2, a % HALF : a % HALF + z - a]
-            nc.scalar.activation(target.bitcast(F32), looked_up(t, V + a, V + z), ACT.Copy)
+        for a, z, b_from in ((0, FIRST_CUT, VECTOR_SHARE_0), (FIRST_CUT, V, V + FIRST_CUT)):
+            vector_gather(loose[:, a : min(z, VECTOR_SHARE_0)], 0, a, min(z, VECTOR_SHARE_0))
+            scalar_gather(loose[:, b_from : V + z], 0, b_from, V + z)
+            nc.gpsimd.tensor_tensor(halves(early[:, a:z], 0), loose[:, a:z], loose[:, V + a : V + z], ADD)
 
         for a in (0, HALF):
-            vector_words(0, a, a + HALF)
-            scalar_words(0, V + a, V + a + HALF)
-            sum_even_plane(0, a, a + HALF, first[:, 0, V + a : V + a + HALF])
+            vector_gather(halves(high_words[:, a : a + HALF], 1), 3, a, a + HALF)
+        scalar_gather(early[:, high_second : high_second + HALF].bitcast(F32), 3, V, V + HALF)
+        scalar_gather(late[:, :HALF].bitcast(F32), 1, V + HALF, S)
+        for a in (HALF, HALF + CHUNK):
+            scalar_gather(late[:, a : a + CHUNK].bitcast(F32), 3, V + a, V + a + CHUNK)
 
-        vector_words(2, 0, VECTOR_SHARE_2)
-        scalar_words(2, VECTOR_SHARE_2, V + HALF)
-        sum_even_plane(2, 0, HALF, first[:, 1, V : V + HALF])
-        parked = second[1][:].rearrange("p u v -> p (u v)")[:, PARKED_AT : PARKED_AT + HALF]
-        nc.scalar.activation(parked.bitcast(F32), looked_up(2, V + HALF, S), ACT.Copy)
-        sum_even_plane(2, HALF, V, parked)
-
-        for t in (1, 3):
-            for a in (0, HALF):
-                vector_high_halves(t, a, a + HALF)
-        for t, a, z in ((1, 0, HALF), (3, 0, HALF), (1, HALF, V), (3, HALF, 3 * CHUNK), (3, 3 * CHUNK, V)):
-            scalar_second_piece(t, a, z)
+        def word_pairs(tile, low, high):
+            rows = tile[:].rearrange("p (r v) -> p r v", v=CHUNK)[:, low // CHUNK : high // CHUNK + 1 : (high - low) // CHUNK, :]
+            return rows.bitcast(BF16).rearrange("p u (c i e) -> p c u i e", i=2, e=2)
 
         sums = [pool.tile([P, 4 * CHUNK], BF16, name="sum_%d" % c, align_bytes=64) for c in range(4)]
         codes = [pool.tile([P, CHUNK], U32, name="codes_%d" % c, align_bytes=64) for c in range(4)]
@@ -106,9 +102,9 @@ def tile_picked_hash_lin_silu_sub_l_kernel(tc, xT, w_words, w_scales, b, offs, o
             return results[:, a:z]
 
         def add(c):
-            a, z = c * CHUNK, (c + 1) * CHUNK
-            pieces = (first[:, :, a:z], second[a // HALF][:, :, a % HALF : a % HALF + CHUNK])
-            rows = [words.bitcast(BF16).rearrange("p u (c i e) -> p c u i e", i=2, e=2) for words in pieces]
+            a = c * CHUNK
+            second = word_pairs(early, low_second + a, high_second + a) if a < HALF else word_pairs(late, a - HALF, a)
+            rows = (word_pairs(early, low_first + a, high_first + a), second)
             nc.vector.tensor_tensor(sums[c][:].rearrange("p (i c u e) -> p c u i e", i=2, u=2, e=2), rows[0], rows[1], ADD)
 
         def finish(c):

@@ -20,7 +20,6 @@ S = D * V
 CHUNK = 128
 HALF = V // 2
 VECTOR_SHARE_1 = 384
-VECTOR_SHARE_0 = 512
 FIRST_CUT = 224
 
 
@@ -55,7 +54,7 @@ def tile_picked_hash_lin_silu_sub_l_kernel(tc, xT, w_words, w_scales, b, offs, o
 
         early = pool.tile([P, 12 * CHUNK], U32, name="early")
         late = pool.tile([P, V], U32, name="late")
-        loose = pool.tile([P, S], BF16, name="loose")
+        loose = pool.tile([P, S], U32, name="loose")
         low_first, low_second, high_second, high_first = 0, V, V + HALF, S
 
         def looked_up(t, a, z):
@@ -78,10 +77,10 @@ def tile_picked_hash_lin_silu_sub_l_kernel(tc, xT, w_words, w_scales, b, offs, o
         vector_gather(early[:, :VECTOR_SHARE_1].bitcast(F32), 1, 0, VECTOR_SHARE_1)
         scalar_gather(early[:, VECTOR_SHARE_1 : V + HALF].bitcast(F32), 1, VECTOR_SHARE_1, V + HALF)
 
-        for a, z, b_from in ((0, FIRST_CUT, VECTOR_SHARE_0), (FIRST_CUT, V, V + FIRST_CUT)):
-            vector_gather(loose[:, a : min(z, VECTOR_SHARE_0)], 0, a, min(z, VECTOR_SHARE_0))
-            scalar_gather(loose[:, b_from : V + z], 0, b_from, V + z)
-            nc.gpsimd.tensor_tensor(halves(early[:, a:z], 0), loose[:, a:z], loose[:, V + a : V + z], ADD)
+        for a, z in ((0, FIRST_CUT), (FIRST_CUT, V)):
+            vector_gather(loose[:, a:z].bitcast(F32), 0, a, z)
+            scalar_gather(loose[:, V + a : V + z].bitcast(F32), 0, V + a, V + z)
+            nc.gpsimd.tensor_tensor(halves(early[:, a:z], 0), halves(loose[:, a:z], 1), halves(loose[:, V + a : V + z], 1), ADD)
 
         for a in (0, HALF):
             vector_gather(halves(high_words[:, a : a + HALF], 1), 3, a, a + HALF)
@@ -92,7 +91,7 @@ def tile_picked_hash_lin_silu_sub_l_kernel(tc, xT, w_words, w_scales, b, offs, o
 
         def word_pairs(tile, low, high):
             rows = tile[:].rearrange("p (r v) -> p r v", v=CHUNK)[:, low // CHUNK : high // CHUNK + 1 : (high - low) // CHUNK, :]
-            return rows.bitcast(BF16).rearrange("p u (c i e) -> p c u i e", i=2, e=2)
+            return rows.bitcast(BF16).rearrange("p u (v e) -> p v u e", e=2)
 
         sums = [pool.tile([P, 4 * CHUNK], BF16, name="sum_%d" % c, align_bytes=64) for c in range(4)]
         codes = [pool.tile([P, CHUNK], U32, name="codes_%d" % c, align_bytes=64) for c in range(4)]
@@ -105,7 +104,7 @@ def tile_picked_hash_lin_silu_sub_l_kernel(tc, xT, w_words, w_scales, b, offs, o
             a = c * CHUNK
             second = word_pairs(early, low_second + a, high_second + a) if a < HALF else word_pairs(late, a - HALF, a)
             rows = (word_pairs(early, low_first + a, high_first + a), second)
-            nc.vector.tensor_tensor(sums[c][:].rearrange("p (i c u e) -> p c u i e", i=2, u=2, e=2), rows[0], rows[1], ADD)
+            nc.vector.tensor_tensor(sums[c][:].rearrange("p (v u e) -> p v u e", u=2, e=2), rows[0], rows[1], ADD)
 
         def finish(c):
             a, z = c * CHUNK, (c + 1) * CHUNK
@@ -116,8 +115,7 @@ def tile_picked_hash_lin_silu_sub_l_kernel(tc, xT, w_words, w_scales, b, offs, o
                 out=acc[:], lhsT=w_codes[:].bitcast(FP8X4), lhsT_scale=w_scale[:],
                 rhs=codes[c][:].bitcast(FP8X4), rhs_scale=scale[:], start=True, stop=True,
             )
-            by_id = acc[:].rearrange("p (i c) -> p c i", i=2)
-            nc.scalar.activation(result(a, z).rearrange("p (c i) -> p c i", i=2), by_id, ACT.Silu, bias=bias[:])
+            nc.scalar.activation(result(a, z), acc[:], ACT.Silu, bias=bias[:])
 
         def store(a, z):
             nc.sync.dma_start(out[:, a:z], result(a, z))

@@ -46,7 +46,8 @@ def tile_picked_hash_lin_silu_sub_l_kernel(tc, xT, w_words, w_scales, b, offs, o
             nc.sync.dma_start(raw[t][:], planes[:, t, :])
 
         w_codes = pool.tile([P, N], U32, name="w_codes", align_bytes=64)
-        nc.sync.dma_start(w_codes[:].bitcast(I32), w_words[0].rearrange("p n r -> p (n r)").bitcast(I32))
+        for a in (0, N // 2):
+            nc.sync.dma_start(w_codes[:, a : a + N // 2].bitcast(I32), w_words[0].rearrange("p n r -> p (n r)").bitcast(I32)[:, a : a + N // 2])
         for q in range(4):
             nc.sync.dma_start(w_scale[32 * q : 32 * q + 4, :].bitcast(I32), w_scales[0, 4 * q : 4 * q + 4, :].bitcast(I32))
         bias = pool.tile([P, 1], F32, name="bias")
@@ -123,9 +124,10 @@ def tile_picked_hash_lin_silu_sub_l_kernel(tc, xT, w_words, w_scales, b, offs, o
         add(0)
         add(1)
         finish(0)
+        store(0, CHUNK)
         add(2)
         finish(1)
-        store(0, HALF)
+        store(CHUNK, HALF)
         add(3)
         for c in (2, 3):
             finish(c)

@@ -19,7 +19,7 @@ P = 128
 S = D * V
 CHUNK = 128
 HALF = V // 2
-VECTOR_SHARE_1 = 384
+VECTOR_SHARE_0 = 384
 FIRST_CUT = 224
 
 
@@ -42,7 +42,7 @@ def tile_picked_hash_lin_silu_sub_l_kernel(tc, xT, w_words, w_scales, b, offs, o
         raw = [pool.tile([P, T], F32, name="raw%d" % t) for t in range(4)]
         nc.sync.dma_start(raw[2][:], planes[:, 2, :])
         nc.sync.dma_start(offsets[:], offs)
-        for t in (1, 0, 3):
+        for t in (0, 1, 3):
             nc.sync.dma_start(raw[t][:], planes[:, t, :])
 
         w_codes = pool.tile([P, N], U32, name="w_codes", align_bytes=64)
@@ -75,13 +75,13 @@ def tile_picked_hash_lin_silu_sub_l_kernel(tc, xT, w_words, w_scales, b, offs, o
         scalar_gather(late[:].bitcast(F32), 2, V, S)
         nc.gpsimd.tensor_tensor(halves(high_words, 0), halves(high_words, 1), halves(late[:], 1), ADD)
 
-        vector_gather(early[:, :VECTOR_SHARE_1].bitcast(F32), 1, 0, VECTOR_SHARE_1)
-        scalar_gather(early[:, VECTOR_SHARE_1 : V + HALF].bitcast(F32), 1, VECTOR_SHARE_1, V + HALF)
+        vector_gather(loose[:, :VECTOR_SHARE_0].bitcast(F32), 0, 0, VECTOR_SHARE_0)
+        scalar_gather(loose[:, VECTOR_SHARE_0:].bitcast(F32), 0, VECTOR_SHARE_0, S)
 
         for a, z in ((0, FIRST_CUT), (FIRST_CUT, V)):
-            vector_gather(loose[:, a:z].bitcast(F32), 0, a, z)
-            scalar_gather(loose[:, V + a : V + z].bitcast(F32), 0, V + a, V + z)
+            vector_gather(early[:, a:z].bitcast(F32), 1, a, z)
             nc.gpsimd.tensor_tensor(halves(early[:, a:z], 0), halves(loose[:, a:z], 1), halves(loose[:, V + a : V + z], 1), ADD)
+        scalar_gather(early[:, low_second : low_second + HALF].bitcast(F32), 1, V, V + HALF)
 
         for a in (0, HALF):
             vector_gather(halves(high_words[:, a : a + HALF], 1), 3, a, a + HALF)

@@ -38,6 +38,9 @@ def tile_picked_hash_lin_silu_sub_l_kernel(tc, xT, w_words, w_scales, b, offs, o
         nc.vector.memset(warm_in[:], 0.0)
         nc.vector.memset(w_scale[:].bitcast(I32), 0)
         nc.scalar.activation(warm_out[:], warm_in[:], ACT.Silu)
+        warm_sum = pool.tile([P, 1], BF16, name="warm_sum")
+        warm_half = warm_in[:].bitcast(BF16)[:, 1:2]
+        nc.gpsimd.tensor_tensor(warm_sum[:], warm_half, warm_half, ADD)
 
         raw = [pool.tile([P, T], F32, name="raw%d" % t) for t in range(4)]
         nc.sync.dma_start(raw[2][:], planes[:, 2, :])

@@ -21,6 +21,9 @@ CHUNK = 128
 HALF = V // 2
 VECTOR_SHARE_0 = 384
 FIRST_CUT = 224
+VECTOR_SHARE_1 = 480
+EARLY = HALF
+CUTS = (0, CHUNK, EARLY, EARLY + CHUNK, V - CHUNK // 2, V)
 
 
 def tile_picked_hash_lin_silu_sub_l_kernel(tc, xT, w_words, w_scales, b, offs, out):
@@ -56,10 +59,10 @@ def tile_picked_hash_lin_silu_sub_l_kernel(tc, xT, w_words, w_scales, b, offs, o
         bias = pool.tile([P, 1], F32, name="bias")
         nc.sync.dma_start(bias[:], b)
 
-        early = pool.tile([P, 12 * CHUNK], U32, name="early")
-        late = pool.tile([P, V], U32, name="late")
+        early = pool.tile([P, 2 * (V + 2 * EARLY) + V], U32, name="early")
+        late = pool.tile([P, V + CHUNK], U32, name="late")
         loose = pool.tile([P, S], U32, name="loose")
-        low_first, low_second, high_second, high_first = 0, V, V + HALF, S
+        low_first, low_second, high_second, high_first = 0, V, V + EARLY, V + 2 * EARLY
 
         def looked_up(t, a, z):
             return raw[t][:].indirect(offsets[:, a // 16 : z // 16])
@@ -75,63 +78,65 @@ def tile_picked_hash_lin_silu_sub_l_kernel(tc, xT, w_words, w_scales, b, offs, o
 
         high_words = early[:, high_first : high_first + V]
         vector_gather(high_words.bitcast(F32), 2, 0, V)
-        scalar_gather(late[:].bitcast(F32), 2, V, S)
-        nc.gpsimd.tensor_tensor(halves(high_words, 0), halves(high_words, 1), halves(late[:], 1), ADD)
+        scalar_gather(late[:, :V].bitcast(F32), 2, V, S)
+        nc.gpsimd.tensor_tensor(halves(high_words, 0), halves(high_words, 1), halves(late[:, :V], 1), ADD)
 
         vector_gather(loose[:, :VECTOR_SHARE_0].bitcast(F32), 0, 0, VECTOR_SHARE_0)
         scalar_gather(loose[:, VECTOR_SHARE_0:].bitcast(F32), 0, VECTOR_SHARE_0, S)
 
-        for a, z in ((0, FIRST_CUT), (FIRST_CUT, V)):
+        for a, z in ((0, FIRST_CUT), (FIRST_CUT, VECTOR_SHARE_1)):
             vector_gather(early[:, a:z].bitcast(F32), 1, a, z)
+        scalar_gather(early[:, VECTOR_SHARE_1 : low_second + EARLY].bitcast(F32), 1, VECTOR_SHARE_1, V + EARLY)
+        for a, z in ((0, FIRST_CUT), (FIRST_CUT, V)):
             nc.gpsimd.tensor_tensor(halves(early[:, a:z], 0), halves(loose[:, a:z], 1), halves(loose[:, V + a : V + z], 1), ADD)
-        scalar_gather(early[:, low_second : low_second + HALF].bitcast(F32), 1, V, V + HALF)
 
-        for a in (0, HALF):
-            vector_gather(halves(high_words[:, a : a + HALF], 1), 3, a, a + HALF)
-        scalar_gather(early[:, high_second : high_second + HALF].bitcast(F32), 3, V, V + HALF)
-        scalar_gather(late[:, :HALF].bitcast(F32), 1, V + HALF, S)
-        for a in (HALF, HALF + CHUNK):
-            scalar_gather(late[:, a : a + CHUNK].bitcast(F32), 3, V + a, V + a + CHUNK)
+        for a, z in ((0, EARLY), (EARLY, V)):
+            vector_gather(halves(high_words[:, a:z], 1), 3, a, z)
+        scalar_gather(early[:, high_second : high_second + EARLY].bitcast(F32), 3, V, V + EARLY)
+        for a, ends in ((EARLY, CUTS[3:4]), (EARLY + CHUNK, CUTS[4:])):
+            low = 2 * (a - EARLY)
+            scalar_gather(late[:, low : low + CHUNK].bitcast(F32), 1, V + a, V + a + CHUNK)
+            for i, j in zip((a,) + ends, ends):
+                scalar_gather(late[:, low + CHUNK + i - a : low + CHUNK + j - a].bitcast(F32), 3, V + i, V + j)
 
-        def word_pairs(tile, low, high):
-            rows = tile[:].rearrange("p (r v) -> p r v", v=CHUNK)[:, low // CHUNK : high // CHUNK + 1 : (high - low) // CHUNK, :]
+        def word_pairs(tile, low, high, n):
+            rows = tile[:, low : 2 * high - low].rearrange("p (u v) -> p u v", u=2)[:, :, :n]
             return rows.bitcast(BF16).rearrange("p u (v e) -> p v u e", e=2)
 
-        sums = [pool.tile([P, 4 * CHUNK], BF16, name="sum_%d" % c, align_bytes=64) for c in range(4)]
-        codes = [pool.tile([P, CHUNK], U32, name="codes_%d" % c, align_bytes=64) for c in range(4)]
+        sums = pool.tile([P, 4 * V], BF16, name="sums", align_bytes=64)
         results = pool.tile([P, V], F32, name="results")
 
-        def result(a, z):
-            return results[:, a:z]
-
         def add(c):
-            a = c * CHUNK
-            second = word_pairs(early, low_second + a, high_second + a) if a < HALF else word_pairs(late, a - HALF, a)
-            rows = (word_pairs(early, low_first + a, high_first + a), second)
-            nc.vector.tensor_tensor(sums[c][:].rearrange("p (v u e) -> p v u e", u=2, e=2), rows[0], rows[1], ADD)
+            a, z = CUTS[c], CUTS[c + 1]
+            first = word_pairs(early, low_first + a, high_first + a, z - a)
+            if a < EARLY:
+                second = word_pairs(early, low_second + a, high_second + a, z - a)
+            else:
+                low = (a - EARLY) // CHUNK * CHUNK + a - EARLY
+                second = word_pairs(late, low, low + CHUNK, z - a)
+            nc.vector.tensor_tensor(sums[:, 4 * a : 4 * z].rearrange("p (v u e) -> p v u e", u=2, e=2), first, second, ADD)
 
         def finish(c):
-            a, z = c * CHUNK, (c + 1) * CHUNK
-            scale = pool.tile([P, CHUNK], U8, name="scale_%d" % c, align_bytes=64)
-            nc.vector.quantize_mx(out=codes[c][:].bitcast(FP8X4), scales=scale[:], in_=sums[c][:])
-            acc = psum.tile([P, CHUNK], F32, name="acc_%d" % c)
+            a, z = CUTS[c], CUTS[c + 1]
+            codes = pool.tile([P, z - a], U32, name="codes_%d" % c, align_bytes=64)
+            scale = pool.tile([P, z - a], U8, name="scale_%d" % c, align_bytes=64)
+            nc.vector.quantize_mx(out=codes[:].bitcast(FP8X4), scales=scale[:], in_=sums[:, 4 * a : 4 * z])
+            acc = psum.tile([P, z - a], F32, name="acc_%d" % c)
             nc.tensor.matmul_mx(
                 out=acc[:], lhsT=w_codes[:].bitcast(FP8X4), lhsT_scale=w_scale[:],
-                rhs=codes[c][:].bitcast(FP8X4), rhs_scale=scale[:], start=True, stop=True,
+                rhs=codes[:].bitcast(FP8X4), rhs_scale=scale[:], start=True, stop=True,
             )
-            nc.scalar.activation(result(a, z), acc[:], ACT.Silu, bias=bias[:])
+            nc.scalar.activation(results[:, a:z], acc[:], ACT.Silu, bias=bias[:])
 
         def store(a, z):
-            nc.sync.dma_start(out[:, a:z], result(a, z))
+            nc.sync.dma_start(out[:, a:z], results[:, a:z])
 
         add(0)
-        add(1)
-        finish(0)
-        store(0, CHUNK)
-        add(2)
-        finish(1)
-        store(CHUNK, HALF)
-        add(3)
-        for c in (2, 3):
+        for c in range(3):
+            add(c + 1)
             finish(c)
-            store(c * CHUNK, (c + 1) * CHUNK)
+            store(CUTS[c], CUTS[c + 1])
+        add(4)
+        finish(3)
+        finish(4)
+        store(CUTS[3], V)

@@ -17,13 +17,11 @@ ADD = mybir.AluOpType.add
 
 P = 128
 S = D * V
-CHUNK = 128
-HALF = V // 2
-VECTOR_SHARE_0 = 384
-FIRST_CUT = 224
-VECTOR_SHARE_1 = 480
-EARLY = HALF
-CUTS = (0, CHUNK, EARLY, EARLY + CHUNK, V - CHUNK // 2, V)
+LAST_PLANE = 2
+VECTOR_SHARES = ((1, 480), (3, 480), (0, 512))
+VECTOR_CUTS = (0, 128, 384)
+SCALAR_CUTS = (0, 128, 256, 384, 448, V)
+CHUNK_CUTS = (0, 128, 256, 384, 448, V)
 
 
 def tile_picked_hash_lin_silu_sub_l_kernel(tc, xT, w_words, w_scales, b, offs, out):
@@ -41,14 +39,11 @@ def tile_picked_hash_lin_silu_sub_l_kernel(tc, xT, w_words, w_scales, b, offs, o
         nc.vector.memset(warm_in[:], 0.0)
         nc.vector.memset(w_scale[:].bitcast(I32), 0)
         nc.scalar.activation(warm_out[:], warm_in[:], ACT.Silu)
-        warm_sum = pool.tile([P, 1], BF16, name="warm_sum")
-        warm_half = warm_in[:].bitcast(BF16)[:, 1:2]
-        nc.gpsimd.tensor_tensor(warm_sum[:], warm_half, warm_half, ADD)
 
         raw = [pool.tile([P, T], F32, name="raw%d" % t) for t in range(4)]
-        nc.sync.dma_start(raw[2][:], planes[:, 2, :])
+        nc.sync.dma_start(raw[1][:], planes[:, 1, :])
         nc.sync.dma_start(offsets[:], offs)
-        for t in (0, 1, 3):
+        for t in (3, 0, LAST_PLANE):
             nc.sync.dma_start(raw[t][:], planes[:, t, :])
 
         w_codes = pool.tile([P, N], U32, name="w_codes", align_bytes=64)
@@ -59,65 +54,42 @@ def tile_picked_hash_lin_silu_sub_l_kernel(tc, xT, w_words, w_scales, b, offs, o
         bias = pool.tile([P, 1], F32, name="bias")
         nc.sync.dma_start(bias[:], b)
 
-        early = pool.tile([P, 2 * (V + 2 * EARLY) + V], U32, name="early")
-        late = pool.tile([P, V + CHUNK], U32, name="late")
-        loose = pool.tile([P, S], U32, name="loose")
-        low_first, low_second, high_second, high_first = 0, V, V + EARLY, V + 2 * EARLY
+        words = pool.tile([P, 2 * S], U32, name="words")
 
-        def looked_up(t, a, z):
-            return raw[t][:].indirect(offsets[:, a // 16 : z // 16])
+        def gather(engine, t, a, z):
+            row = words[:, (t // 2) * S + a : (t // 2) * S + z]
+            if t % 2 == 1:
+                to = row.bitcast(F32)
+            else:
+                to = row.bitcast(BF16).rearrange("p (j e) -> p j e", e=2)[:, :, 0]
+            looked_up = raw[t][:].indirect(offsets[:, a // 16 : z // 16])
+            if engine is nc.vector:
+                nc.vector.tensor_copy(to, looked_up)
+            else:
+                nc.scalar.activation(to, looked_up, ACT.Copy)
 
-        def halves(words, e):
-            return words.bitcast(BF16).rearrange("p (j e) -> p j e", e=2)[:, :, e]
+        for t, share in VECTOR_SHARES:
+            gather(nc.vector, t, 0, share)
+            gather(nc.scalar, t, share, S)
 
-        def vector_gather(to, t, a, z):
-            nc.vector.tensor_copy(to, looked_up(t, a, z))
-
-        def scalar_gather(to, t, a, z):
-            nc.scalar.activation(to, looked_up(t, a, z), ACT.Copy)
-
-        high_words = early[:, high_first : high_first + V]
-        vector_gather(high_words.bitcast(F32), 2, 0, V)
-        scalar_gather(late[:, :V].bitcast(F32), 2, V, S)
-        nc.gpsimd.tensor_tensor(halves(high_words, 0), halves(high_words, 1), halves(late[:, :V], 1), ADD)
-
-        vector_gather(loose[:, :VECTOR_SHARE_0].bitcast(F32), 0, 0, VECTOR_SHARE_0)
-        scalar_gather(loose[:, VECTOR_SHARE_0:].bitcast(F32), 0, VECTOR_SHARE_0, S)
-
-        for a, z in ((0, FIRST_CUT), (FIRST_CUT, VECTOR_SHARE_1)):
-            vector_gather(early[:, a:z].bitcast(F32), 1, a, z)
-        scalar_gather(early[:, VECTOR_SHARE_1 : low_second + EARLY].bitcast(F32), 1, VECTOR_SHARE_1, V + EARLY)
-        for a, z in ((0, FIRST_CUT), (FIRST_CUT, V)):
-            nc.gpsimd.tensor_tensor(halves(early[:, a:z], 0), halves(loose[:, a:z], 1), halves(loose[:, V + a : V + z], 1), ADD)
-
-        for a, z in ((0, EARLY), (EARLY, V)):
-            vector_gather(halves(high_words[:, a:z], 1), 3, a, z)
-        scalar_gather(early[:, high_second : high_second + EARLY].bitcast(F32), 3, V, V + EARLY)
-        for a, ends in ((EARLY, CUTS[3:4]), (EARLY + CHUNK, CUTS[4:])):
-            low = 2 * (a - EARLY)
-            scalar_gather(late[:, low : low + CHUNK].bitcast(F32), 1, V + a, V + a + CHUNK)
-            for i, j in zip((a,) + ends, ends):
-                scalar_gather(late[:, low + CHUNK + i - a : low + CHUNK + j - a].bitcast(F32), 3, V + i, V + j)
-
-        def word_pairs(tile, low, high, n):
-            rows = tile[:, low : 2 * high - low].rearrange("p (u v) -> p u v", u=2)[:, :, :n]
-            return rows.bitcast(BF16).rearrange("p u (v e) -> p v u e", e=2)
+        for a, z in zip(VECTOR_CUTS, VECTOR_CUTS[1:]):
+            gather(nc.vector, LAST_PLANE, a, z)
+        for a, z in zip(SCALAR_CUTS, SCALAR_CUTS[1:]):
+            if a == VECTOR_CUTS[-1]:
+                gather(nc.scalar, LAST_PLANE, a, V)
+            gather(nc.scalar, LAST_PLANE, V + a, V + z)
 
         sums = pool.tile([P, 4 * V], BF16, name="sums", align_bytes=64)
         results = pool.tile([P, V], F32, name="results")
 
         def add(c):
-            a, z = CUTS[c], CUTS[c + 1]
-            first = word_pairs(early, low_first + a, high_first + a, z - a)
-            if a < EARLY:
-                second = word_pairs(early, low_second + a, high_second + a, z - a)
-            else:
-                low = (a - EARLY) // CHUNK * CHUNK + a - EARLY
-                second = word_pairs(late, low, low + CHUNK, z - a)
+            a, z = SCALAR_CUTS[c], SCALAR_CUTS[c + 1]
+            pairs = words[:].bitcast(BF16).rearrange("p (u j e) -> p j u e", u=2, e=2)
+            first, second = pairs[:, a:z], pairs[:, V + a : V + z]
             nc.vector.tensor_tensor(sums[:, 4 * a : 4 * z].rearrange("p (v u e) -> p v u e", u=2, e=2), first, second, ADD)
 
         def finish(c):
-            a, z = CUTS[c], CUTS[c + 1]
+            a, z = CHUNK_CUTS[c], CHUNK_CUTS[c + 1]
             codes = pool.tile([P, z - a], U32, name="codes_%d" % c, align_bytes=64)
             scale = pool.tile([P, z - a], U8, name="scale_%d" % c, align_bytes=64)
             nc.vector.quantize_mx(out=codes[:].bitcast(FP8X4), scales=scale[:], in_=sums[:, 4 * a : 4 * z])
@@ -135,8 +107,8 @@ def tile_picked_hash_lin_silu_sub_l_kernel(tc, xT, w_words, w_scales, b, offs, o
         for c in range(3):
             add(c + 1)
             finish(c)
-            store(CUTS[c], CUTS[c + 1])
+            store(CHUNK_CUTS[c], CHUNK_CUTS[c + 1])
         add(4)
         finish(3)
         finish(4)
-        store(CUTS[3], V)
+        store(CHUNK_CUTS[3], V)

@@ -18,8 +18,9 @@ ADD = mybir.AluOpType.add
 P = 128
 S = D * V
 LAST_PLANE = 2
-VECTOR_SHARES = ((1, 480), (3, 480), (0, 512))
-VECTOR_CUTS = (0, 128, 384)
+WIDE = 1280
+VECTOR_SHARES = ((1, 576), (3, 384), (0, 544))
+VECTOR_CUTS = (0, 256, 384)
 SCALAR_CUTS = (0, 128, 256, 384, 448, V)
 CHUNK_CUTS = (0, 128, 256, 384, 448, V)
 
@@ -40,11 +41,11 @@ def tile_picked_hash_lin_silu_sub_l_kernel(tc, xT, w_words, w_scales, b, offs, o
         nc.vector.memset(w_scale[:].bitcast(I32), 0)
         nc.scalar.activation(warm_out[:], warm_in[:], ACT.Silu)
 
-        raw = [pool.tile([P, T], F32, name="raw%d" % t) for t in range(4)]
+        raw = [pool.tile([P, WIDE if t == 3 else T], F32, name="raw%d" % t) for t in range(4)]
         nc.sync.dma_start(raw[1][:], planes[:, 1, :])
         nc.sync.dma_start(offsets[:], offs)
         for t in (3, 0, LAST_PLANE):
-            nc.sync.dma_start(raw[t][:], planes[:, t, :])
+            nc.sync.dma_start(raw[t][:, :T], planes[:, t, :])
 
         w_codes = pool.tile([P, N], U32, name="w_codes", align_bytes=64)
         for a in (0, N // 2):
@@ -58,10 +59,10 @@ def tile_picked_hash_lin_silu_sub_l_kernel(tc, xT, w_words, w_scales, b, offs, o
 
         def gather(engine, t, a, z):
             row = words[:, (t // 2) * S + a : (t // 2) * S + z]
-            if t % 2 == 1:
+            if t == 1 and engine is nc.vector:
                 to = row.bitcast(F32)
             else:
-                to = row.bitcast(BF16).rearrange("p (j e) -> p j e", e=2)[:, :, 0]
+                to = row.bitcast(BF16).rearrange("p (j e) -> p j e", e=2)[:, :, t % 2]
             looked_up = raw[t][:].indirect(offsets[:, a // 16 : z // 16])
             if engine is nc.vector:
                 nc.vector.tensor_copy(to, looked_up)

@@ -18,8 +18,8 @@ ADD = mybir.AluOpType.add
 P = 128
 S = D * V
 LAST_PLANE = 2
-WIDE = 1280
-VECTOR_SHARES = ((1, 576), (3, 384), (0, 544))
+WIDE = 1152
+VECTOR_SHARES = ((1, 544), (3, 448), (0, 512))
 VECTOR_CUTS = (0, 256, 384)
 SCALAR_CUTS = (0, 128, 256, 384, 448, V)
 CHUNK_CUTS = (0, 128, 256, 384, 448, V)
@@ -59,7 +59,7 @@ def tile_picked_hash_lin_silu_sub_l_kernel(tc, xT, w_words, w_scales, b, offs, o
 
         def gather(engine, t, a, z):
             row = words[:, (t // 2) * S + a : (t // 2) * S + z]
-            if t == 1 and engine is nc.vector:
+            if t % 2 == 1 and engine is nc.vector:
                 to = row.bitcast(F32)
             else:
                 to = row.bitcast(BF16).rearrange("p (j e) -> p j e", e=2)[:, :, t % 2]

@@ -18,7 +18,6 @@ ADD = mybir.AluOpType.add
 P = 128
 S = D * V
 LAST_PLANE = 2
-WIDE = 1152
 VECTOR_SHARES = ((1, 544), (3, 448), (0, 512))
 VECTOR_CUTS = (0, 256, 384)
 SCALAR_CUTS = (0, 128, 256, 384, 448, V)
@@ -41,11 +40,11 @@ def tile_picked_hash_lin_silu_sub_l_kernel(tc, xT, w_words, w_scales, b, offs, o
         nc.vector.memset(w_scale[:].bitcast(I32), 0)
         nc.scalar.activation(warm_out[:], warm_in[:], ACT.Silu)
 
-        raw = [pool.tile([P, WIDE if t == 3 else T], F32, name="raw%d" % t) for t in range(4)]
+        raw = [pool.tile([P, T], F32, name="raw%d" % t) for t in range(4)]
         nc.sync.dma_start(raw[1][:], planes[:, 1, :])
         nc.sync.dma_start(offsets[:], offs)
         for t in (3, 0, LAST_PLANE):
-            nc.sync.dma_start(raw[t][:, :T], planes[:, t, :])
+            nc.sync.dma_start(raw[t][:], planes[:, t, :])
 
         w_codes = pool.tile([P, N], U32, name="w_codes", align_bytes=64)
         for a in (0, N // 2):
@@ -59,10 +58,10 @@ def tile_picked_hash_lin_silu_sub_l_kernel(tc, xT, w_words, w_scales, b, offs, o
 
         def gather(engine, t, a, z):
             row = words[:, (t // 2) * S + a : (t // 2) * S + z]
-            if t % 2 == 1 and engine is nc.vector:
+            if t % 2 == 1:
                 to = row.bitcast(F32)
             else:
-                to = row.bitcast(BF16).rearrange("p (j e) -> p j e", e=2)[:, :, t % 2]
+                to = row.bitcast(BF16).rearrange("p (j e) -> p j e", e=2)[:, :, 0]
             looked_up = raw[t][:].indirect(offsets[:, a // 16 : z // 16])
             if engine is nc.vector:
                 nc.vector.tensor_copy(to, looked_up)

from contextlib import ExitStack

import concourse.mybir as mybir

K, T, D, V, N = 512, 1024, 2, 512, 128
FLOPS = 2 * K * V * N

F32 = mybir.dt.float32
BF16 = mybir.dt.bfloat16
I32 = mybir.dt.int32
U32 = mybir.dt.uint32
U16 = mybir.dt.uint16
U8 = mybir.dt.uint8
FP8X4 = mybir.dt.float8_e4m3fn_x4
ACT = mybir.ActivationFunctionType
ADD = mybir.AluOpType.add

P = 128
S = D * V
LAST_PLANE = 2
VECTOR_SHARES = ((1, 544), (3, 448), (0, 512))
VECTOR_CUTS = (0, 256, 384)
SCALAR_CUTS = (0, 128, 256, 384, 448, V)
CHUNK_CUTS = (0, 128, 256, 384, 448, V)


def tile_picked_hash_lin_silu_sub_l_kernel(tc, xT, w_words, w_scales, b, offs, out):
    nc = tc.nc
    with ExitStack() as ctx:
        pool = ctx.enter_context(tc.tile_pool(name="held", bufs=1))
        psum = ctx.enter_context(tc.psum_pool(name="psum", bufs=1))

        planes = xT.rearrange("(p t) c -> p t c", t=4)
        offsets = pool.tile([P, S // 16], U16, name="offsets")

        warm_in = pool.tile([P, 1], F32, name="warm_in")
        warm_out = pool.tile([P, 1], F32, name="warm_out")
        w_scale = pool.tile([P, N], U8, name="w_scale", align_bytes=64)
        nc.vector.memset(warm_in[:], 0.0)
        nc.vector.memset(w_scale[:].bitcast(I32), 0)
        nc.scalar.activation(warm_out[:], warm_in[:], ACT.Silu)

        raw = [pool.tile([P, T], F32, name="raw%d" % t) for t in range(4)]
        nc.sync.dma_start(raw[1][:], planes[:, 1, :])
        nc.sync.dma_start(offsets[:], offs)
        for t in (3, 0, LAST_PLANE):
            nc.sync.dma_start(raw[t][:], planes[:, t, :])

        w_codes = pool.tile([P, N], U32, name="w_codes", align_bytes=64)
        for a in (0, N // 2):
            nc.sync.dma_start(w_codes[:, a : a + N // 2].bitcast(I32), w_words[0].rearrange("p n r -> p (n r)").bitcast(I32)[:, a : a + N // 2])
        for q in range(4):
            nc.sync.dma_start(w_scale[32 * q : 32 * q + 4, :].bitcast(I32), w_scales[0, 4 * q : 4 * q + 4, :].bitcast(I32))
        bias = pool.tile([P, 1], F32, name="bias")
        nc.sync.dma_start(bias[:], b)

        words = pool.tile([P, 2 * S], U32, name="words")

        def gather(engine, t, a, z):
            row = words[:, (t // 2) * S + a : (t // 2) * S + z]
            if t % 2 == 1:
                to = row.bitcast(F32)
            else:
                to = row.bitcast(BF16).rearrange("p (j e) -> p j e", e=2)[:, :, 0]
            looked_up = raw[t][:].indirect(offsets[:, a // 16 : z // 16])
            if engine is nc.vector:
                nc.vector.tensor_copy(to, looked_up)
            else:
                nc.scalar.activation(to, looked_up, ACT.Copy)

        for t, share in VECTOR_SHARES:
            gather(nc.vector, t, 0, share)
            gather(nc.scalar, t, share, S)

        for a, z in zip(VECTOR_CUTS, VECTOR_CUTS[1:]):
            gather(nc.vector, LAST_PLANE, a, z)
        for a, z in zip(SCALAR_CUTS, SCALAR_CUTS[1:]):
            if a == VECTOR_CUTS[-1]:
                gather(nc.scalar, LAST_PLANE, a, V)
            gather(nc.scalar, LAST_PLANE, V + a, V + z)

        sums = pool.tile([P, 4 * V], BF16, name="sums", align_bytes=64)
        results = pool.tile([P, V], F32, name="results")

        def add(c):
            a, z = SCALAR_CUTS[c], SCALAR_CUTS[c + 1]
            pairs = words[:].bitcast(BF16).rearrange("p (u j e) -> p j u e", u=2, e=2)
            first, second = pairs[:, a:z], pairs[:, V + a : V + z]
            nc.vector.tensor_tensor(sums[:, 4 * a : 4 * z].rearrange("p (v u e) -> p v u e", u=2, e=2), first, second, ADD)

        def finish(c):
            a, z = CHUNK_CUTS[c], CHUNK_CUTS[c + 1]
            codes = pool.tile([P, z - a], U32, name="codes_%d" % c, align_bytes=64)
            scale = pool.tile([P, z - a], U8, name="scale_%d" % c, align_bytes=64)
            nc.vector.quantize_mx(out=codes[:].bitcast(FP8X4), scales=scale[:], in_=sums[:, 4 * a : 4 * z])
            acc = psum.tile([P, z - a], F32, name="acc_%d" % c)
            nc.tensor.matmul_mx(
                out=acc[:], lhsT=w_codes[:].bitcast(FP8X4), lhsT_scale=w_scale[:],
                rhs=codes[:].bitcast(FP8X4), rhs_scale=scale[:], start=True, stop=True,
            )
            nc.scalar.activation(results[:, a:z], acc[:], ACT.Silu, bias=bias[:])

        def store(a, z):
            nc.sync.dma_start(out[:, a:z], results[:, a:z])

        add(0)
        for c in range(3):
            add(c + 1)
            finish(c)
            store(CHUNK_CUTS[c], CHUNK_CUTS[c + 1])
        add(4)
        finish(3)
        finish(4)
        store(CHUNK_CUTS[3], V)
